import numpy as np, ml_dtypes
CORES = [10,34,74,98]
N = 4
BF = ml_dtypes.bfloat16
def gentries(a):
    return np.ascontiguousarray(a.reshape(8, 16, -1).transpose(0, 2, 1)).reshape(8, -1)
def gtable(e):
    e = np.asarray(e); return np.ascontiguousarray(e.reshape(8, -1, 16).transpose(0, 2, 1)).reshape(128, -1).astype(np.int32)
M, B, H, ST = 224, 16, 4, 4
W = M * B
def parts(rng):
    c = np.minimum((W * np.exp2(-5 * rng.random((N, 8, 1, W))) * rng.random((N, 8, 16, W))).astype(np.int64), W - 1)
    a = np.exp2(5 * rng.random((N, 8, 16, 1))); q = rng.choice(np.array([1, 1, 1, 16, 256]), (N, 8, 16, 1))
    l = np.minimum((W * rng.random((N, 8, 16, W)) ** a).astype(np.int64), W - 1) & -q
    gap = np.minimum((W * (0.1 + 0.8 * rng.random((N, 8, 1, M))) * (0.5 + rng.random((N, 8, 16, M)))).astype(np.int64), W - 1)
    return c, l, gap, rng.integers(0, B, (N, 8, M))
def pack(c, l, gap, cur):
    return {"ck": np.ascontiguousarray(c.reshape(N, 128, W)).astype(np.int32), "la": np.ascontiguousarray(l.reshape(N, 128, W)).astype(np.int32),
            "gap": np.ascontiguousarray(gap.reshape(N, 128, M)).astype(np.int32), "cu": np.stack([gtable(a) for a in cur])}
def setup_inputs(rng):
    return pack(*parts(rng))
def setup_inputs_ties(rng):
    c, l, gap, cur = parts(rng); c = c & -64; gap = gap & -64; l = l & -64
    kind = rng.integers(0, 4, (N, 8, 16, 1)); kind[:, :, :4, 0] = np.arange(4)
    few = np.take_along_axis(rng.integers(0, W, (N, 8, 16, 4)), rng.integers(0, kind + 1, (N, 8, 16, W)), 3)
    l[:, ::2] = few[:, ::2]
    gap = np.where((rng.random((N, 8, 1, M)) < 0.25) & (rng.random((N, 8, 16, M)) < 0.2), 0, gap)
    return pack(c, l, gap, cur)
def setup_inputs_alike(rng):
    c, l, gap, cur = parts(rng)
    c[:, ::2] = np.maximum(c[:, ::2, :1], 16); c[:, ::2, :, 0] = rng.integers(0, 16, (N, 4, 16))
    c[:, 1::2] = rng.choice(np.array([3, W // 3, W // 2, W - 1]), (N, 4, 16, W))
    cur[:, :, 0] = 0; gap[:, :, :, 0] = 0
    return pack(c, l, gap, cur)
def setup_inputs_ends(rng):
    c, l, gap, cur = parts(rng)
    c[:, 0:4] = rng.choice(np.array([0, 1, W - 2, W - 1]), (N, 4, 16, W))
    l[:, 2:6] = rng.choice(np.array([0, 1, W - 2, W - 1]), (N, 4, 16, W))
    gap[:, 1:7] = rng.choice(np.array([0, 1, W - 1]), (N, 6, 16, M))
    cur = rng.choice(np.array([0, B - 1]), (N, 8, M))
    return pack(c, l, gap, cur)
def setup_inputs_count(rng):
    c, l, gap, cur = parts(rng); c = np.maximum(c, 1)
    n = rng.choice(np.array([0, H - 1, H, H + 1, 16]), (N, 8, 1, M)); g = rng.permutation(8)
    n[:, g[0]] = 16; n[:, g[1]] = 0; n[:, g[2], 0, :5] = np.array([0, H - 1, H, H + 1, 16])
    cur[:, g[0], :B] = np.arange(B)
    n[0::2, g[3]] = 16; n[1::2, g[3]] = 0
    n[:, g[4]] = 16; l[:, g[4]] = l[:, g[4], :, :1].copy(); c[:, g[4], :, 0] = 0
    cur[:, g[4], 0] = 1; cur[:, g[4], 1:9] = (2 * np.arange(N)[:, None] + np.arange(8)) & (B - 1)
    gap = np.where(np.argsort(rng.random((N, 8, 16, M)), axis=2) < n, 0, W - 1)
    return pack(c, l, gap, cur)
def setup_inputs_spread(rng):
    c, l, gap, cur = parts(rng); e = np.log2(W)
    c = np.minimum((np.exp2(e * rng.random((N, 8, 1, W))) * rng.random((N, 8, 16, W))).astype(np.int64), W - 1)
    l = np.minimum(np.exp2(e * rng.random((N, 8, 16, W)) ** (2 * rng.random((N, 8, 16, 1)))).astype(np.int64), W - 1)
    gap = np.minimum((np.exp2(e * (1 - rng.random((N, 8, 1, M)) ** 3)) * rng.random((N, 8, 16, M))).astype(np.int64), W - 1)
    return pack(c, l, gap, cur)
def check_inputs(d):
    bad = []
    for k, hi in (("ck", W - 1), ("la", W - 1), ("gap", W - 1), ("cu", B - 1)):
        if np.min(d[k]) < 0 or np.max(d[k]) > hi: bad.append("range of " + k)
    return bad
def columns(t, x):
    return np.take_along_axis(t, np.swapaxes(x, 2, 3).reshape(N, 8, 1, 16 * M), 3).reshape(N, 8, 16, M, 16)
def reference(ck, la, gap, cu):
    C = ck.astype(np.int64).reshape(N, 8, 16, W); L = la.astype(np.int64).reshape(N, 8, 16, W); G = gap.astype(np.int64).reshape(N, 8, 16, M)
    cur = np.stack([gentries(a) for a in cu]).astype(np.int64); first = B * np.arange(M)
    I = np.take_along_axis(C, (first + cur)[:, :, None, :], 3); T = I + G
    for step in range(ST):
        A = columns(L, I); top = np.max(A, axis=4, keepdims=True)
        s = np.max(np.where(A < top, A, 0), axis=4)
        I = np.maximum(I, np.max(columns(C, s), axis=4))
        out = np.add.reduce((I >= T).astype(np.int64), axis=2) >= H
        hit = (np.arange(B) == cur[..., None]) & out[..., None]
        C = np.where(hit[:, :, None], I[..., None], C.reshape(N, 8, 16, M, B)).reshape(N, 8, 16, W)
        cur = np.where(out, (cur + 1) & (B - 1), cur)
        new = np.take_along_axis(C, (first + cur)[:, :, None, :], 3)
        T = np.where(out[:, :, None], new + G, T); I = np.where(out[:, :, None], new, I)
        I, T, G, cur = np.roll(I, 1, axis=0), np.roll(T, 1, axis=0), np.roll(G, 1, axis=0), np.roll(cur, 1, axis=0)
    return {"yi": I.reshape(N, 128, M).astype(np.float32), "yc": np.stack([gtable(a) for a in cur]).astype(np.float32)}

@@ -1,0 +1,460 @@
+import math
+from concourse.bass import DstId, RemoteDMATransfer
+from concourse.mybir import dt, AluOpType, AxisListType, ActivationFunctionType
+
+W = 3584
+M = 224
+ST = 4
+NQ = 14
+SIZES = [64, 64, 64, 32]
+CHUNKS = []
+_a = 0
+for _n in SIZES:
+    CHUNKS.append((_a, _a + _n))
+    _a += _n
+NC = len(CHUNKS)
+CP = [(16 * _x, 16 * _y) for _x, _y in CHUNKS]
+LP = [(896 * _x, 896 * _x + 896) for _x in range(4)]
+KE = 512.0
+KV = float(2 ** 60)
+SC = 32.0 / math.log(2.0)
+B0 = -100.0 * math.log(2.0)
+UP = 2.0 ** 50
+OFF = 1600.0
+EPS = 2.0 ** -62
+CW, CT, CR, CE = 32, 48, 272, 496
+
+SCRATCH = {}
+
+
+def _declare():
+    def sb(names, n, t):
+        for x in names.split():
+            SCRATCH[x] = ("sbuf", [128, n], t)
+
+    sb("ck32 la32", W, "int32")
+    sb("cf lf", W, "float32")
+    sb("Cc", 2 * W, "bfloat16")
+    sb("Lc", W, "bfloat16")
+    sb("cu32 il32 rl32 pt pa q16 cl c16", NQ, "int32")
+    sb("ni nw", 28, "int32")
+    sb("gap32 yint", M, "int32")
+    sb("gapf gc0 gc1 gc2 lnI lnS yout", M, "float32")
+    sb("il rl", NQ, "uint16")
+    sb("Iu su", M, "uint16")
+    sb("Inew Rld R s2", M, "bfloat16")
+    sb("pm", 42, "float32")
+    sb("lst", 28, "uint16")
+    sb("mask", 1024, "bfloat16")
+    sb("fK fN idK idN fP fQ bP1 bP bQ1 bQ hP hQ f1 id1", 128, "bfloat16")
+    sb("fF idF", 128, "float32")
+    sb("fE e1 e2 e3", 144, "bfloat16")
+    for t in range(ST + 1):
+        sb("Ic%d" % t, M, "bfloat16")
+        sb("TW%d" % t, CE, "float32")
+    for t in range(ST):
+        sb("MS%d" % t, CR, "float32")
+        sb("IP%d" % t, M, "bfloat16")
+    for j, n in enumerate(SIZES):
+        sb("x%d y%d P%d u%d z%d q%d" % (j, j, j, j, j, j), n * 16, "bfloat16")
+    for k in range(8):
+        SCRATCH["ps%d" % k] = ("psum", [128, 512], "float32")
+
+
+_declare()
+BANKS = []
+_b = 0
+for _n in SIZES:
+    _k = -(-_n * 16 // 512)
+    BANKS.append([(_b + _i) % 8 for _i in range(_k)])
+    _b += _k
+CB = 7
+
+SEMAPHORES = ["vec", "act", "ten", "gps", "loc", "gap"]
+for _t in range(ST):
+    SEMAPHORES += ["a%d_%d" % (_t, _j) for _j in range(NC)] + ["b%d" % _t]
+SEMAPHORES += ["ld%d" % _k for _k in range(len(CP) + len(LP) + 2)] + ["st%d" % _k for _k in range(NC + 1)]
+
+COST = {"cy": 0.83e-3, "gather": 1.4, "scatter": 3.0, "fix": 0.03, "gfix": 0.07, "lat": 0.05, "net": 2.0, "send": 0.9,
+        "mm": 0.046, "ld0": 2.0, "ld": 1.4, "tab": 1.5}
+NUDGE = {}
+for _w in ("scan2_2:-6 min1_0:-1 lnS2:-5 diff1_1:7 scan3_3:5 lnS0:5 diff2_0:-5 min3_0:-2 scan3_1:-4 s2_0:2 gapc:6 vote2:8 min2_1:-7 G1_2:-6 min1_1:8 "
+           "count:7 n3:2 n4:-2 scan2_3:-2 G2_1:-7 n1:6 decS0:1 s1_0:2 Iu0:-5 scan3_0:-3 Tr:-6").split():
+    NUDGE[_w.split(":")[0]] = float(_w.split(":")[1])
+
+
+def dur(ck, c):
+    k, n = ck
+    if k == "v":
+        return c["fix"] + max(64, n) * c["cy"]
+    if k == "s":
+        return c["gfix"] + max(32, n) * c["cy"]
+    if k == "stab":
+        return c["tab"] + c["gfix"] + n * c["cy"]
+    if k == "gather":
+        return c["gfix"] + n * c["gather"] * c["cy"]
+    if k == "scatter":
+        return c["gfix"] + n * c["scatter"] * c["cy"]
+    if k == "mm":
+        return n * c["mm"]
+    if k == "sel":
+        return 0.2 + 2 * n * c["cy"]
+    if k == "ld":
+        return c["ld0"] + n * c["ld"]
+    if k == "us":
+        return n
+    return n * c[k]
+
+
+def plan(ops, c=COST, nudge=NUDGE):
+    n = len(ops)
+    cost = [dur(o["ck"], c) for o in ops]
+    lat = c["lat"]
+    succ = [[] for _ in range(n)]
+    for i, o in enumerate(ops):
+        for d in o["deps"]:
+            succ[d].append(i)
+    prio = [0.0] * n
+    for i in range(n - 1, -1, -1):
+        best = 0.0
+        for k in succ[i]:
+            best = max(best, prio[k] + lat)
+        prio[i] = cost[i] + best
+    prio = [p + nudge.get(o["name"], 0.0) for p, o in zip(prio, ops)]
+    left = [len(o["deps"]) for o in ops]
+    est = [0.0] * n
+    ready = [i for i in range(n) if left[i] == 0]
+    fin = [0.0] * n
+    free = {}
+    order = []
+    beg = [0.0] * n
+    while ready:
+        pick, key = None, None
+        for i in ready:
+            q = ops[i]["q"]
+            s = est[i] if q == "X" else max(est[i], free.get(q, 0.0))
+            if key is None or (s, -prio[i]) < key:
+                pick, key = i, (s, -prio[i])
+        q = ops[pick]["q"]
+        ready.remove(pick)
+        order.append(pick)
+        beg[pick] = key[0]
+        fin[pick] = key[0] + cost[pick]
+        if q != "X":
+            free[q] = fin[pick]
+        for k in succ[pick]:
+            left[k] -= 1
+            est[k] = max(est[k], fin[pick] + lat)
+            if left[k] == 0:
+                ready.append(k)
+    return order, beg, fin
+
+
+def build(g, T, topo, core, rank):
+    A, F = AluOpType, ActivationFunctionType
+    ops = []
+    hist = {}
+
+    def op(q, ck, fn, reads=(), writes=(), sem=None, deps=(), kind="c", name=""):
+        i = len(ops)
+        dd = set(deps)
+        for lst, wr in ((reads, False), (writes, True)):
+            for (b, lo, hi) in lst:
+                for (l2, h2, k, w2) in hist.get(b, ()):
+                    if k != i and l2 < hi and lo < h2 and (wr or w2):
+                        dd.add(k)
+        for (b, lo, hi) in writes:
+            h = hist.get(b, [])
+            hist[b] = [e for e in h if not (lo <= e[0] and e[1] <= hi)] + [(lo, hi, i, True)]
+        for (b, lo, hi) in reads:
+            hist.setdefault(b, []).append((lo, hi, i, False))
+        ops.append({"q": q, "ck": ck, "fn": fn, "deps": dd, "sem": sem, "kind": kind, "name": name})
+        return i
+
+    def V(n, fn, reads, writes, name=""):
+        return op("V", ("v", n), fn, reads, writes, name=name)
+
+    def S(n, fn, reads, writes, name="", deps=(), k="s"):
+        return op("S", (k, n), fn, reads, writes, name=name, deps=deps)
+
+    def SG(n, fn, reads, writes, name=""):
+        return op("S", ("gather", n), fn, reads, writes, name=name)
+
+    def full(b):
+        return (b, 0, 1 << 20)
+
+    v, sc, te, sy = g.vector, g.scalar, g.tensor, g.sync
+
+    for b, c in (("fK", KE), ("fN", -KE), ("fP", KV), ("fQ", -KV), ("fE", 1.0), ("hP", -3.5 * KV), ("hQ", 3.5 * KV), ("f1", 1.0), ("fF", 1.0), ("mask", 1.0)):
+        V(512 if b == "mask" else 64, lambda b=b, c=c: v.memset(T[b][:], c), [], [full(b)], "fill")
+    V(64, lambda: v.memset(T.mask[:, 0::16], 0.0), [], [full("mask")], "mask")
+    for t in range(ST):
+        V(64, lambda t=t: v.memset(T["MS%d" % t][:, CW:CT], 0.0), [], [("MS%d" % t, CW, CT)], "MSpad")
+
+    def sel(out, src, n, pattern, cmp, base, cm):
+        op("G", ("sel", n), lambda: g.affine_select(T[out][:], T[src][:], pattern, cmp, 0.0, base, cm), [full(src)], [full(out)], name="sel")
+
+    op("G", ("us", 0.2), lambda: g.iota(T.pt[:], [[0, NQ]], 0, 1), [], [full("pt")], name="iota")
+    op("G", ("us", 0.2), lambda: g.iota(T.q16[:], [[16, NQ]], 0, 0), [], [full("q16")], name="iota")
+    for o, f in (("idN", "fN"), ("idK", "fK"), ("idF", "fF"), ("id1", "f1")):
+        sel(o, f, 128, [[-1, 128]], A.is_equal, 0, 1)
+    for x in "PQ":
+        sel("b" + x + "1", "f" + x, 128, [[-16, 8], [0, 16]], A.is_ge, 0, 1)
+        sel("b" + x, "b" + x + "1", 128, [[16, 8], [0, 16]], A.is_ge, 15, -1)
+    sel("e1", "fE", 144, [[0, 9], [1, 16]], A.is_equal, -15, 0)
+    sel("e2", "e1", 144, [[-16, 9], [0, 16]], A.is_ge, 0, 1)
+    sel("e3", "e2", 144, [[16, 9], [0, 16]], A.is_ge, 15, -1)
+
+    V(NQ, lambda: v.tensor_scalar(T.pa[:], T.pt[:], 15, None, A.bitwise_and), [full("pt")], [full("pa")])
+    V(NQ, lambda: v.tensor_tensor(T.cl[:], T.pa[:], T.q16[:], A.add), [full("pa"), full("q16")], [full("cl")])
+    V(NQ, lambda: v.tensor_scalar(T.c16[:], T.cl[:], 16.0, None, A.mult), [full("cl")], [full("c16")])
+    for t in range(ST - 1):
+        b = "TW%d" % t
+        V(NQ, lambda b=b: v.tensor_scalar(T[b][:, 18:32], T.cl[:], 1.0, None, A.mult), [full("cl")], [(b, 18, 32)])
+
+    dq = {"Y": sy, "S": sc}
+    nld = [0]
+    amount = [0]
+
+    def load(q, out, in_, b, lo, hi):
+        k = nld[0]
+        nld[0] += 1
+        amount[0] += hi - lo
+        i = op(q, ("us", 0.06), lambda: dq[q].dma_start(out, in_), [], [], sem="ld%d" % k, kind="dma", name="ld")
+        op("X", ("ld", amount[0] / 896.0), None, [], [(b, lo, hi)], sem=("ld%d" % k, 16), kind="arr", deps=[i], name="land")
+
+    def load_c(q, p):
+        lo, hi = CP[p]
+        load(q, T.ck32[:, lo:hi], T.ck[:, lo:hi], "ck32", lo, hi)
+
+    def load_l(q, p):
+        lo, hi = LP[p]
+        load(q, T.la32[:, lo:hi], T.la[:, lo:hi], "la32", lo, hi)
+
+    load("Y", T.cu32[:], T.cu[:], "cu32", 0, NQ)
+    load_c("Y", 0)
+    load_l("S", 0)
+    load_l("Y", 1)
+    load_l("S", 2)
+    load_l("Y", 3)
+    load_c("S", 1)
+    load("Y", T.gap32[:], T.gap[:], "gap32", 0, M)
+    load_c("S", 2)
+    load_c("Y", 3)
+
+    V(NQ, lambda: v.tensor_copy(T.TW0[:, CW:CW + NQ], T.cu32[:]), [full("cu32")], [("TW0", CW, CW + NQ)])
+    V(NQ, lambda: v.tensor_tensor(T.il32[:], T.cu32[:], T.c16[:], A.add), [full("cu32"), full("c16")], [full("il32")])
+    V(NQ, lambda: v.tensor_copy(T.il[:], T.il32[:]), [full("il32")], [full("il")])
+    for a, e in CHUNKS:
+        op("V", ("gather", e - a), lambda a=a, e=e: v.tensor_copy(T.Iu[:, a:e], T.ck32[:, 0:16 * e].indirect(T.il[:, a // 16:e // 16])),
+           [("ck32", 0, 16 * e), full("il")], [("Iu", a, e)], name="Iu0")
+    exps = []
+
+    def encode(src, f, o, lo, hi, q, k="s"):
+        if q == "V":
+            V(hi - lo, lambda: v.tensor_copy(T[f][:, lo:hi], T[src][:, lo:hi]), [(src, lo, hi)], [(f, lo, hi)], "conv")
+        else:
+            op("G", ("sel", hi - lo), lambda: g.affine_select(T[f][:, lo:hi], T[src][:, lo:hi], [[0, hi - lo]], A.is_ge, 0.0, 0, 0), [(src, lo, hi)], [(f, lo, hi)], name="convg")
+        exps.append(S(hi - lo, lambda: sc.activation(T[o][:, lo:hi], T[f][:, lo:hi], F.Exp, bias=B0, scale=1.0 / SC), [(f, lo, hi)], [(o, lo, hi)], name="exp", k=k))
+
+    encode("ck32", "cf", "Cc", CP[0][0], CP[0][1], "V", "stab")
+    for lo, hi in LP:
+        encode("la32", "lf", "Lc", lo, hi, "V")
+    for lo, hi in CP[1:]:
+        encode("ck32", "cf", "Cc", lo, hi, "G")
+    V(M, lambda: v.tensor_scalar(T.gapf[:], T.gap32[:], 0.5, None, A.subtract), [full("gap32")], [full("gapf")])
+    exps.append(S(M, lambda: sc.activation(T.gc0[:], T.gapf[:], F.Exp, scale=1.0 / SC), [full("gapf")], [full("gc0")], name="expg"))
+
+    nloc = [0]
+    cores = list(T.cores)
+    nxt = cores[(rank + 1) % len(cores)]
+
+    def send_gap():
+        dst = [cores[(rank + d) % len(cores)] for d in (1, 2)]
+        eng = [e for e in topo.engines(core, dst[0]) if e in topo.engines(core, dst[1])]
+        m = 0
+        for e in eng:
+            m |= 1 << e
+        ids = []
+        for d in dst:
+            a = topo.addr(d)
+            ids.append(DstId(rid=a[0], pnc=a[1]))
+        nloc[0] += len(eng)
+        g.remote_dma_fused([RemoteDMATransfer(dst_ids=ids, dma_engine_mask=m, remote_sem=T.sem.gap, srcs=[T.gc0[:]], dsts=[T.gc1[:], T.gc2[:]])], local_sem=T.sem.loc)
+
+    i = op("G", ("send", 1), send_gap, [full("gc0")], [], kind="send", name="gap")
+    ne = len(topo.engines(core, nxt))
+    op("X", ("us", 5.0), None, [], [full("gc1"), full("gc2")], sem=("gap", 2 * ne), kind="arr", deps=[i], name="agap")
+
+    def send(out, in_, sem):
+        a = topo.addr(nxt)
+        nloc[0] += ne
+        g.remote_dma(out, in_, T.sem[sem], T.sem.loc, a[1], a[0], topo.mask(core, nxt))
+
+    cn = "ps%d" % CB
+    pc = T[cn]
+    SG(M, lambda: sc.activation(T.Ic0[:], T.Cc[:, 0:W].indirect(T.il[:]), F.Copy), [("Cc", 0, W), full("il")], [full("Ic0")], name="Ic0")
+
+    def step(t):
+        last = t == ST - 1
+        IC, TW, MS, IP = "Ic%d" % t, "TW%d" % t, "MS%d" % t, "IP%d" % t
+        Icb, TWb, MSb, IPb = T[IC], T[TW], T[MS], T[IP]
+        if not last:
+            gb = "gc%d" % t
+            op("P", ("mm", 14), lambda: te.matmul(pc[:, 16:240], T.idF[:], T[gb][:], True, True), [full("idF"), full(gb)], [full(cn)], name="gapc")
+            if t == 0:
+                V(M, lambda: v.tensor_tensor(TWb[:, CT:CR], T.Ic0[:], pc[:, 16:240], A.mult), [full("Ic0"), full(cn)], [("TW0", CT, CR)], "Tc0")
+        for j, (a, e) in enumerate(CHUNKS):
+            n = e - a
+            xb, yb, Pb, ub = T["x%d" % j], T["y%d" % j], T["P%d" % j], T["u%d" % j]
+            X, Y, P, U = "x%d" % j, "y%d" % j, "P%d" % j, "u%d" % j
+            if t > 0:
+                S(n, lambda a=a, e=e: sc.activation(T.lnI[:, a:e], Icb[:, a:e], F.Ln, scale=UP), [(IC, a, e)], [("lnI", a, e)], name="lnI%d" % j)
+                V(n, lambda a=a, e=e: v.tensor_scalar(T.Iu[:, a:e], T.lnI[:, a:e], SC, OFF + 0.25, A.mult, A.add), [("lnI", a, e)], [("Iu", a, e)], "decI%d" % j)
+            SG(16 * n, lambda a=a, e=e, xb=xb: sc.activation(xb[:], T.Lc[:].indirect(T.Iu[:, a:e]), F.Copy), [full("Lc"), ("Iu", a, e)], [full(X)], name="G1_%d" % j)
+            V(8 * n, lambda n=n, xb=xb, Pb=Pb: v.tensor_tensor_scan(Pb[:], T.mask[:, 0:16 * n], xb[:], 0.0, A.mult, A.max), [full("mask"), full(X)], [full(P)], "scan1_%d" % j)
+            bk = BANKS[j]
+            per = 16 // len(bk)
+            for h, b in enumerate(bk):
+                def diff(n=n, xb=xb, Pb=Pb, h=h, k=len(bk), per=per, pb=T["ps%d" % b]):
+                    te.matmul(pb[:, 0:per * n], T.idN[:], xb[:, h::k], True, False)
+                    for i in range(per):
+                        r = te.matmul(pb[:, i:per * n:per], T.idK[:], Pb[:, 15::16], False, i == per - 1)
+                    return r
+
+                op("P", ("mm", per + per * n / 64), diff, [full("idK"), full("idN"), full(P), full(X)], [full("ps%d" % b)], name="diff%d_%d" % (j, h))
+                V(per * n, lambda n=n, xb=xb, yb=yb, h=h, k=len(bk), per=per, pb=T["ps%d" % b]: v.tensor_tensor(yb[:, h::k], xb[:, h::k], pb[:, 0:per * n], A.min),
+                  [full(X), full("ps%d" % b)], [(Y, h, h + 1)], "min%d_%d" % (j, h))
+            V(8 * n, lambda n=n, yb=yb, ub=ub: v.tensor_tensor_scan(ub[:], T.mask[:, 0:16 * n], yb[:], 0.0, A.mult, A.max), [full("mask"), full(Y)], [full(U)], "scan2_%d" % j)
+            S(n, lambda a=a, e=e, ub=ub: sc.activation(T.lnS[:, a:e], ub[:, 15::16], F.Ln, bias=EPS, scale=UP), [full(U)], [("lnS", a, e)],
+              deps=exps if t == 0 else (), name="lnS%d" % j, k="stab" if t == 0 and j == 0 else "s")
+            V(n, lambda a=a, e=e: v.tensor_scalar(T.su[:, a:e], T.lnS[:, a:e], SC, OFF + 0.25, A.mult, A.add), [("lnS", a, e)], [("su", a, e)], "decS%d" % j)
+        V(NQ, lambda: v.tensor_copy(T.ni[:, 0:14], TWb[:, CW:CW + NQ]), [(TW, CW, CW + NQ)], [("ni", 0, 14)], "n0")
+        V(NQ, lambda: v.tensor_scalar(T.ni[:, 14:28], TWb[:, CW:CW + NQ], 1.0, None, A.add), [(TW, CW, CW + NQ)], [("ni", 14, 28)], "n1")
+        V(NQ, lambda: v.tensor_scalar(T.nw[:], T.ni[:], 15, None, A.bitwise_and), [full("ni")], [full("nw")], "n2")
+        V(NQ, lambda: v.tensor_tensor(T.rl32[:], T.nw[:, 14:28], T.c16[:], A.add), [full("nw"), full("c16")], [full("rl32")], "n3")
+        V(NQ, lambda: v.tensor_copy(T.rl[:], T.rl32[:]), [full("rl32")], [full("rl")], "n4")
+        if not last:
+            V(NQ, lambda: v.tensor_tensor(TWb[:, 4:18], T.nw[:, 0:14], T.c16[:], A.add), [full("nw"), full("c16")], [(TW, 4, 18)], "n5")
+        SG(M, lambda: sc.activation(T.Rld[:], T.Cc[:, 0:W].indirect(T.rl[:]), F.Copy), [("Cc", 0, W), full("rl")], [full("Rld")], name="Rld")
+        if not last:
+            V(M, lambda: v.tensor_tensor(TWb[:, CR:CE], T.Rld[:], pc[:, 16:240], A.mult), [full("Rld"), full(cn)], [(TW, CR, CE)], "Tr")
+        for j, (a, e) in enumerate(CHUNKS):
+            n = e - a
+            zb, qb = T["z%d" % j], T["q%d" % j]
+            Z, Q = "z%d" % j, "q%d" % j
+            pn, qn = "ps%d" % BANKS[j][0], "ps%d" % BANKS[j][-1]
+            pb, qp = T[pn], T[qn]
+
+            def prep(a=a, e=e, n=n, qp=qp):
+                te.matmul(qp[:, 256:256 + n], T.id1[:], Icb[:, a:e], True, True)
+                return te.matmul(qp[:, 320:320 + n], T.idF[:], TWb[:, CT + a:CT + e], True, True)
+
+            op("P", ("mm", 5), prep, [full("id1"), full("idF"), (IC, a, e), (TW, CT + a, CT + e)], [full(qn)], name="prep%d" % j)
+            SG(16 * n, lambda a=a, e=e, zb=zb: sc.activation(zb[:], T.Cc[:, 0:W].indirect(T.su[:, a:e]), F.Copy), [("Cc", 0, W), ("su", a, e)], [full(Z)], name="G2_%d" % j)
+            V(8 * n, lambda n=n, zb=zb, qb=qb: v.tensor_tensor_scan(qb[:], T.mask[:, 0:16 * n], zb[:], 0.0, A.mult, A.max), [full("mask"), full(Z)], [full(Q)], "scan3_%d" % j)
+            V(n, lambda a=a, e=e, n=n, qb=qb, qp=qp: v.tensor_tensor(T.Inew[:, a:e], qb[:, 15::16], qp[:, 256:256 + n], A.max), [full(qn), full(Q)], [("Inew", a, e)], "Inew%d" % j)
+            V(n, lambda a=a, e=e, n=n, qp=qp: v.tensor_tensor(T.R[:, a:e], T.Inew[:, a:e], qp[:, 320:320 + n], A.is_ge), [("Inew", a, e), full(qn)], [("R", a, e)], "R%d" % j)
+
+            def votes(a=a, e=e, n=n, pb=pb):
+                for k, (w, h) in enumerate((("bP", "hP"), ("bQ", "hQ"))):
+                    o = pb[:, k * n:k * n + n]
+                    te.matmul(o, T[w][:], T.R[:, a:e], True, False)
+                    r = te.matmul(o, T[h][0:1, :], T.f1[0:1, 0:n], False, True)
+                return r
+
+            op("P", ("mm", 4), votes, [full("bP"), full("bQ"), full("hP"), full("hQ"), full("f1"), ("R", a, e)], [full(pn)], name="vote%d" % j)
+            V(n, lambda a=a, e=e, n=n, pb=pb: v.tensor_tensor(T.s2[:, a:e], T.Inew[:, a:e], pb[:, n:2 * n], A.min), [("Inew", a, e), full(pn)], [("s2", a, e)], "s2_%d" % j)
+            V(n, lambda a=a, e=e, n=n, pb=pb: v.tensor_tensor(pb[:, 128:128 + n], T.Rld[:, a:e], pb[:, 0:n], A.min), [("Rld", a, e), full(pn)], [full(pn)], "s1_%d" % j)
+            V(n, lambda a=a, e=e, n=n, pb=pb: v.tensor_tensor(IPb[:, a:e], T.s2[:, a:e], pb[:, 128:128 + n], A.max), [full(pn), ("s2", a, e)], [(IP, a, e)], "IP%d" % j)
+            nm = "a%d_%d" % (t, j)
+            i = op("G", ("send", 1), lambda a=a, e=e, nm=nm: send(T["Ic%d" % (t + 1)][:, a:e], IPb[:, a:e], nm), [(IP, a, e)], [], kind="send", name="A%d" % j)
+            op("X", ("net", 1), None, [], [("Ic%d" % (t + 1), a, e)], sem=(nm, ne), kind="arr", deps=[i], name="arrA%d" % j)
+
+        def count():
+            for p in range(16):
+                r = te.matmul(pc[:, 0:NQ], T.e3[:, 15 - p:143 - p], T.R[:, p::16], p == 0, p == 15)
+            return r
+
+        op("P", ("mm", 16), count, [full("e3"), full("R")], [full(cn)], name="count")
+        lo = 28 if last else 0
+        if not last:
+            V(NQ, lambda: v.tensor_scalar(T.pm[:, 0:14], pc[:, 0:NQ], 3.5, float(W), A.is_lt, A.mult), [full(cn)], [("pm", 0, 14)], "c0")
+            V(NQ, lambda: v.tensor_scalar(T.pm[:, 14:28], pc[:, 0:NQ], 3.5, float(M), A.is_ge, A.mult), [full(cn)], [("pm", 14, 28)], "c1")
+        V(NQ, lambda: v.tensor_scalar(T.pm[:, 28:42], pc[:, 0:NQ], 3.5, None, A.is_ge), [full(cn)], [("pm", 28, 42)], "c2")
+        V(42, lambda: v.tensor_tensor(MSb[:, 4 + lo:46], T.pm[:, lo:42], TWb[:, 4 + lo:46], A.add), [("pm", lo, 42), (TW, 4 + lo, 46)], [(MS, 4 + lo, 46)], "c3")
+        if not last:
+            V(28, lambda: v.tensor_copy(T.lst[:], MSb[:, 4:32]), [(MS, 4, 32)], [full("lst")], "c4")
+            SG(M, lambda: sc.activation(MSb[:, CT:CR], TWb[:, CT:CE].indirect(T.lst[:, 14:28]), F.Copy), [(TW, CT, CE), full("lst")], [(MS, CT, CR)], name="Tsel")
+            op("V", ("scatter", M), lambda: v.tensor_copy(T.Cc[:].indirect(T.lst[:, 0:14]), T.Inew[:]), [full("Inew"), full("lst")], [full("Cc")], name="scatter")
+        hi = CT if last else CR
+        i = op("G", ("send", 1), lambda: send(T["TW%d" % (t + 1)][:, CW:hi], MSb[:, CW:hi], "b%d" % t), [(MS, CW, hi)], [], kind="send", name="B")
+        op("X", ("net", 1), None, [], [("TW%d" % (t + 1), CW, hi)], sem=("b%d" % t, ne), kind="arr", deps=[i], name="arrB")
+
+    for t in range(ST):
+        step(t)
+    IC, TW = "Ic%d" % ST, "TW%d" % ST
+    Fb, Lb = T[IC], T[TW]
+    for j, (a, e) in enumerate(CHUNKS):
+        n = e - a
+        S(n, lambda a=a, e=e: sc.activation(T.lnI[:, a:e], Fb[:, a:e], F.Ln, scale=UP), [(IC, a, e)], [("lnI", a, e)], name="lnY")
+        V(n, lambda a=a, e=e: v.tensor_scalar(T.yint[:, a:e], T.lnI[:, a:e], SC, OFF, A.mult, A.add), [("lnI", a, e)], [("yint", a, e)])
+        V(n, lambda a=a, e=e: v.tensor_copy(T.yout[:, a:e], T.yint[:, a:e]), [("yint", a, e)], [("yout", a, e)])
+        op("Y", ("us", 0.1), lambda a=a, e=e: sy.dma_start(T.yi[:, a:e], T.yout[:, a:e]), [("yout", a, e)], [], sem="st%d" % j, kind="dma", name="yi")
+    V(NQ, lambda: v.tensor_copy(T.ni[:, 0:14], Lb[:, CW:CW + NQ]), [(TW, CW, CW + NQ)], [("ni", 0, 14)])
+    V(NQ, lambda: v.tensor_scalar(T.nw[:, 0:14], T.ni[:, 0:14], 15, None, A.bitwise_and), [("ni", 0, 14)], [("nw", 0, 14)])
+    V(NQ, lambda: v.tensor_copy(Lb[:, 4:18], T.nw[:, 0:14]), [("nw", 0, 14)], [(TW, 4, 18)])
+    op("Y", ("us", 0.1), lambda: sy.dma_start(T.yc[:], Lb[:, 4:18]), [(TW, 4, 18)], [], sem="st%d" % NC, kind="dma", name="yc")
+    return ops, nloc
+
+
+SEMOF = {"V": "vec", "S": "act", "P": "ten", "G": "gps"}
+
+
+def emit(g, T, ops, order):
+    eng = {"V": g.vector, "S": g.scalar, "P": g.tensor, "G": g, "Y": g.sync}
+    cnt = {"vec": 0, "act": 0, "ten": 0, "gps": 0}
+    seen = {q: {} for q in eng}
+    tok = {}
+    for i in order:
+        o = ops[i]
+        if o["q"] == "X":
+            tok[i] = (o["sem"][0], o["sem"][1], {o["sem"][0]: o["sem"][1]})
+            continue
+        q = o["q"]
+        s = seen[q]
+        toks = sorted([tok[d] for d in o["deps"] if tok.get(d) is not None], key=lambda x: (-sum(x[2].values()), x[0]))
+        top = {}
+        for sem, val, clock in toks:
+            top[sem] = max(top.get(sem, 0), val)
+        for sem, val, clock in toks:
+            if s.get(sem, 0) >= val or top[sem] > val:
+                continue
+            eng[q].wait_ge(T.sem[sem], val)
+            for k, w in clock.items():
+                s[k] = max(s.get(k, 0), w)
+        r = o["fn"]()
+        tok[i] = None
+        if o["kind"] == "c":
+            sem = SEMOF[q]
+            cnt[sem] += 1
+            r.then_inc(T.sem[sem], 1)
+            c = dict(s)
+            c[sem] = cnt[sem]
+            tok[i] = (sem, cnt[sem], c)
+        elif o["kind"] == "dma":
+            r.then_inc(T.sem[o["sem"]], 16)
+    for sem in sorted(cnt):
+        g.wait_ge(T.sem[sem], cnt[sem])
+
+
+def rank_program(g, core, T, topo):
+    rank = T.rank_of(core)
+    if rank is None:
+        return
+    ops, nloc = build(g, T, topo, core, rank)
+    order, beg, fin = plan(ops)
+    emit(g, T, ops, order)
+    for k in range(NC + 1):
+        g.wait_ge(T.sem["st%d" % k], 16)
+    g.wait_ge(T.sem.loc, nloc[0])

@@ -215,12 +215,14 @@ def build(g, T, topo, core, rank):
     dq = {"Y": sy, "S": sc}
     nld = [0]
     amount = [0]
+    prev = {"Y": [], "S": []}
 
     def load(q, out, in_, b, lo, hi):
         k = nld[0]
         nld[0] += 1
         amount[0] += hi - lo
-        i = op(q, ("us", 0.06), lambda: dq[q].dma_start(out, in_), [], [], sem="ld%d" % k, kind="dma", name="ld")
+        i = op(q, ("us", 0.06), lambda: dq[q].dma_start(out, in_), [], [], sem="ld%d" % k, kind="dma", name="ld", deps=prev[q])
+        prev[q] = [i]
         op("X", ("ld", amount[0] / 896.0), None, [], [(b, lo, hi)], sem=("ld%d" % k, 16), kind="arr", deps=[i], name="land")
 
     def load_c(q, p):
@@ -232,15 +234,12 @@ def build(g, T, topo, core, rank):
         load(q, T.la32[:, lo:hi], T.la[:, lo:hi], "la32", lo, hi)
 
     load("Y", T.cu32[:], T.cu[:], "cu32", 0, NQ)
-    load_c("Y", 0)
-    load_l("S", 0)
-    load_l("Y", 1)
-    load_l("S", 2)
-    load_l("Y", 3)
-    load_c("S", 1)
     load("Y", T.gap32[:], T.gap[:], "gap32", 0, M)
-    load_c("S", 2)
-    load_c("Y", 3)
+    load_c("Y", 0)
+    for p in range(len(LP)):
+        load_l("Y", p)
+    for p in range(1, len(CP)):
+        load_c("Y", p)
 
     V(NQ, lambda: v.tensor_copy(T.TW0[:, CW:CW + NQ], T.cu32[:]), [full("cu32")], [("TW0", CW, CW + NQ)])
     V(NQ, lambda: v.tensor_tensor(T.il32[:], T.cu32[:], T.c16[:], A.add), [full("cu32"), full("c16")], [full("il32")])
@@ -257,13 +256,13 @@ def build(g, T, topo, core, rank):
             op("G", ("sel", hi - lo), lambda: g.affine_select(T[f][:, lo:hi], T[src][:, lo:hi], [[0, hi - lo]], A.is_ge, 0.0, 0, 0), [(src, lo, hi)], [(f, lo, hi)], name="convg")
         exps.append(S(hi - lo, lambda: sc.activation(T[o][:, lo:hi], T[f][:, lo:hi], F.Exp, bias=B0, scale=1.0 / SC), [(f, lo, hi)], [(o, lo, hi)], name="exp", k=k))
 
-    encode("ck32", "cf", "Cc", CP[0][0], CP[0][1], "V", "stab")
+    encode("ck32", "cf", "Cc", CP[0][0], CP[0][1], "V")
     for lo, hi in LP:
         encode("la32", "lf", "Lc", lo, hi, "V")
     for lo, hi in CP[1:]:
         encode("ck32", "cf", "Cc", lo, hi, "G")
     V(M, lambda: v.tensor_scalar(T.gapf[:], T.gap32[:], 0.5, None, A.subtract), [full("gap32")], [full("gapf")])
-    exps.append(S(M, lambda: sc.activation(T.gc0[:], T.gapf[:], F.Exp, scale=1.0 / SC), [full("gapf")], [full("gc0")], name="expg"))
+    exps.append(S(M, lambda: sc.activation(T.gc0[:], T.gapf[:], F.Exp, scale=1.0 / SC), [full("gapf")], [full("gc0")], name="expg", k="stab"))
 
     nloc = [0]
     cores = list(T.cores)

@@ -1,33 +1,65 @@
 import math
 from concourse.bass import DstId, RemoteDMATransfer
-from concourse.mybir import dt, AluOpType, AxisListType, ActivationFunctionType
+from concourse.mybir import AluOpType, ActivationFunctionType
 
 W = 3584
 M = 224
 ST = 4
 NQ = 14
-SIZES = [64, 64, 64, 32]
-CHUNKS = []
-_a = 0
-for _n in SIZES:
-    CHUNKS.append((_a, _a + _n))
-    _a += _n
-NC = len(CHUNKS)
-CP = [(16 * _x, 16 * _y) for _x, _y in CHUNKS]
-LP = [(896 * _x, 896 * _x + 896) for _x in range(4)]
+CYC = ("G2.0 lnI.3 lnS.1 Rld.0 decI.3 G1.3 diff0.2 diff1.2 decS.1 scan3.0 Inew.0 R.0 min0.2 vote.0 s2.0 s1.0 neg0.3 gapc.0 min1.2 scan1.3 scan2.2 neg1.3 "
+       "G2.1 A.0 lnS.2 Tr.0 n0.2 decS.2 scan3.1 diff0.3 prep.1 Inew.1 R.1 diff1.3 col.2 min0.3 "
+       "G2.2 vote.1 s2.1 s1.1 n1.2 lnI.0+ gapc.2 prep.2 min1.3 Rld.2 scan2.3 lnS.3 decI.0+ G1.0+ base.1 Tr.2 scan3.2 prep.3 Inew.2 R.2 count.1 decS.3 c0.1 vote.2 "
+       "s1.2 s2.2 neg1.0+ spread.1 scan1.0+ c2.1 diff1.0+ "
+       "G2.3 A.1 c1.1 lnI.1+ Tsel.1 min1.0+ scan3.3 decI.1+ Inew.3 R.3 base.3 neg0.0+ diff0.0+ count.3 vote.3 scatter.1 min0.0+ c0.3 scan2.0+ s2.3 s1.3 spread.3 "
+       "A.2 B.1 G1.1+ lnI.2+ c2.3 c1.3 Tsel.3 lnS.0+ decI.2+ scan1.1+ decS.0+ scatter.3 G1.2+ neg1.1+ neg0.1+ diff1.1+ min1.1+ diff0.1+ min0.1+ n0.0+ scan2.1+ "
+       "prep.0+ neg0.2+ col.0+ n1.0+ scan1.2+ neg1.2+ A.3 B.3")
+PAR = {
+    "sizes": [48, 64, 64, 48],
+    "halves": [2, 2],
+    "lp": [1024, 1024, 1024, 512],
+    "cp": [48, 64, 32, 32, 32, 16],
+    "lead": 0,
+    "convc": "VGGGVV",
+    "g1v": (2,), "g2v": (),
+    "zq": "SS",
+    "tq": "S", "rq": "S", "uq": "S", "fold": True, "fin": 3,
+    "open": "G1.0 exp.0 G1.1 exp.1 exp.2 exp.4 exp.3 exp.5 lnS.0 G2.0 G2.1 G1.3 G2.2 G2.3",
+    "close": "G2.0 G1.3 G2.1 G2.2 G2.3",
+    "cycle": CYC,
+    "lock": (2,), "weights": [3, 0, 1, 1, 0, 1], "rounds": 70000, "heat": 0.0007, "seed": 1,
+}
 KE = 512.0
 KV = float(2 ** 60)
 SC = 32.0 / math.log(2.0)
-B0 = -100.0 * math.log(2.0)
+SHIFT = 45.0 / 64
+B0 = (SHIFT / 32 - 100.0) * math.log(2.0)
 UP = 2.0 ** 50
-OFF = 1600.0
+OFF = 1600.0 - SHIFT
 EPS = 2.0 ** -62
-CW, CT, CR, CE = 32, 48, 272, 496
+Q = 16
 
 SCRATCH = {}
+SEMAPHORES = []
+LAY = {}
 
 
-def _declare():
+def cuts(sizes):
+    out, a = [], 0
+    for n in sizes:
+        out.append((a, a + n))
+        a += n
+    return out
+
+
+def declare():
+    SCRATCH.clear()
+    chunks = cuts(PAR["sizes"])
+    parts, j = [], 0
+    for k in PAR["halves"]:
+        parts.append((j, j + k, chunks[j][0], chunks[j + k - 1][1]))
+        j += k
+    LAY.update(chunks=chunks, parts=parts, lp=cuts(PAR["lp"]), cp=[(16 * a, 16 * e) for a, e in cuts(PAR["cp"])])
+
     def sb(names, n, t):
         for x in names.split():
             SCRATCH[x] = ("sbuf", [128, n], t)
@@ -36,124 +68,58 @@ def _declare():
     sb("cf lf", W, "float32")
     sb("Cc", 2 * W, "bfloat16")
     sb("Lc", W, "bfloat16")
-    sb("cu32 il32 rl32 pt pa q16 cl c16", NQ, "int32")
-    sb("ni nw", 28, "int32")
-    sb("gap32 yint", M, "int32")
-    sb("gapf gc0 gc1 gc2 lnI lnS yout", M, "float32")
-    sb("il rl", NQ, "uint16")
+    sb("cu32 il32 pt pa q16 cl c16", 2 * Q, "int32")
+    sb("gap32 Ri Ni", M, "int32")
+    sb("gapf gc0 gc1 gc2 lnI lnS lnR f2s", M, "float32")
+    sb("fo fi", M + 2 * Q, "float32")
+    sb("cuin", NQ, "int32")
+    sb("il", 2 * Q, "uint16")
     sb("Iu su", M, "uint16")
-    sb("Inew Rld R s2", M, "bfloat16")
-    sb("pm", 42, "float32")
-    sb("lst", 28, "uint16")
-    sb("mask", 1024, "bfloat16")
-    sb("fK fN idK idN fP fQ bP1 bP bQ1 bQ hP hQ f1 id1", 128, "bfloat16")
-    sb("fF idF", 128, "float32")
-    sb("fE e1 e2 e3", 144, "bfloat16")
-    for t in range(ST + 1):
-        sb("Ic%d" % t, M, "bfloat16")
-        sb("TW%d" % t, CE, "float32")
+    sb("Inew Rld R", M, "bfloat16")
+    sb("mask", 16 * max(PAR["sizes"]), "bfloat16")
+    sb("idK idN bP bQ f1 id1 idW idA idB hb", 128, "bfloat16")
+    sb("idF", 128, "float32")
+    sb("e3", 144, "bfloat16")
+    for h, (j0, j1, a, e) in enumerate(parts):
+        n = e - a
+        sb("ni%d" % h, Q, "float32")
+        sb("nw%d" % h, 2 * Q, "bfloat16")
+        sb("cb%d" % h, 3 * Q, "bfloat16")
+        sb("rl%d" % h, Q, "uint16")
+        sb("ls%d" % h, 2 * Q, "uint16")
+        sb("mm%d" % h, Q, "bfloat16")
+        sb("idH%d" % h, 128, "bfloat16")
+        for t in range(ST):
+            sb("TW%d_%d" % (t, h), 2 * n + 4 * Q, "bfloat16")
+            if t < ST - 1:
+                sb("MS%d_%d" % (t, h), n + 2 * Q, "bfloat16")
     for t in range(ST):
-        sb("MS%d" % t, CR, "float32")
-        sb("IP%d" % t, M, "bfloat16")
-    for j, n in enumerate(SIZES):
+        sb("Ic%d" % t, M, "bfloat16")
+        if t < ST - 1:
+            sb("IP%d s2%d" % (t, t), M, "bfloat16")
+    for j, n in enumerate(PAR["sizes"]):
         sb("x%d y%d P%d u%d z%d q%d" % (j, j, j, j, j, j), n * 16, "bfloat16")
     for k in range(8):
         SCRATCH["ps%d" % k] = ("psum", [128, 512], "float32")
+    s = ["vec", "act", "ten", "gps", "loc", "gap"]
+    for t in range(ST):
+        s += ["a%d_%d" % (t, j) for j in range(len(chunks))] + ["b%d_%d" % (t, h) for h in range(len(parts))]
+    s += ["ld%d" % k for k in range(len(PAR["cp"]) + len(PAR["lp"]) + 2)] + ["st%d" % k for k in range(len(chunks) + 1)]
+    SEMAPHORES[:] = s
 
 
-_declare()
-BANKS = []
-_b = 0
-for _n in SIZES:
-    _k = -(-_n * 16 // 512)
-    BANKS.append([(_b + _i) % 8 for _i in range(_k)])
-    _b += _k
-CB = 7
-
-SEMAPHORES = ["vec", "act", "ten", "gps", "loc", "gap"]
-for _t in range(ST):
-    SEMAPHORES += ["a%d_%d" % (_t, _j) for _j in range(NC)] + ["b%d" % _t]
-SEMAPHORES += ["ld%d" % _k for _k in range(len(CP) + len(LP) + 2)] + ["st%d" % _k for _k in range(NC + 1)]
-
-COST = {"cy": 0.83e-3, "gather": 1.4, "scatter": 3.0, "fix": 0.03, "gfix": 0.07, "lat": 0.05, "net": 2.0, "send": 0.9,
-        "mm": 0.046, "ld0": 2.0, "ld": 1.4, "tab": 1.5}
-NUDGE = {}
-for _w in ("scan2_2:-6 min1_0:-1 lnS2:-5 diff1_1:7 scan3_3:5 lnS0:5 diff2_0:-5 min3_0:-2 scan3_1:-4 s2_0:2 gapc:6 vote2:8 min2_1:-7 G1_2:-6 min1_1:8 "
-           "count:7 n3:2 n4:-2 scan2_3:-2 G2_1:-7 n1:6 decS0:1 s1_0:2 Iu0:-5 scan3_0:-3 Tr:-6").split():
-    NUDGE[_w.split(":")[0]] = float(_w.split(":")[1])
-
-
-def dur(ck, c):
-    k, n = ck
-    if k == "v":
-        return c["fix"] + max(64, n) * c["cy"]
-    if k == "s":
-        return c["gfix"] + max(32, n) * c["cy"]
-    if k == "stab":
-        return c["tab"] + c["gfix"] + n * c["cy"]
-    if k == "gather":
-        return c["gfix"] + n * c["gather"] * c["cy"]
-    if k == "scatter":
-        return c["gfix"] + n * c["scatter"] * c["cy"]
-    if k == "mm":
-        return n * c["mm"]
-    if k == "sel":
-        return 0.2 + 2 * n * c["cy"]
-    if k == "ld":
-        return c["ld0"] + n * c["ld"]
-    if k == "us":
-        return n
-    return n * c[k]
-
-
-def plan(ops, c=COST, nudge=NUDGE):
-    n = len(ops)
-    cost = [dur(o["ck"], c) for o in ops]
-    lat = c["lat"]
-    succ = [[] for _ in range(n)]
-    for i, o in enumerate(ops):
-        for d in o["deps"]:
-            succ[d].append(i)
-    prio = [0.0] * n
-    for i in range(n - 1, -1, -1):
-        best = 0.0
-        for k in succ[i]:
-            best = max(best, prio[k] + lat)
-        prio[i] = cost[i] + best
-    prio = [p + nudge.get(o["name"], 0.0) for p, o in zip(prio, ops)]
-    left = [len(o["deps"]) for o in ops]
-    est = [0.0] * n
-    ready = [i for i in range(n) if left[i] == 0]
-    fin = [0.0] * n
-    free = {}
-    order = []
-    beg = [0.0] * n
-    while ready:
-        pick, key = None, None
-        for i in ready:
-            q = ops[i]["q"]
-            s = est[i] if q == "X" else max(est[i], free.get(q, 0.0))
-            if key is None or (s, -prio[i]) < key:
-                pick, key = i, (s, -prio[i])
-        q = ops[pick]["q"]
-        ready.remove(pick)
-        order.append(pick)
-        beg[pick] = key[0]
-        fin[pick] = key[0] + cost[pick]
-        if q != "X":
-            free[q] = fin[pick]
-        for k in succ[pick]:
-            left[k] -= 1
-            est[k] = max(est[k], fin[pick] + lat)
-            if left[k] == 0:
-                ready.append(k)
-    return order, beg, fin
+declare()
 
 
 def build(g, T, topo, core, rank):
     A, F = AluOpType, ActivationFunctionType
+    chunks, parts, LP, CP = LAY["chunks"], LAY["parts"], LAY["lp"], LAY["cp"]
+    NC = len(chunks)
+    FIN = PAR["fin"]
+    YC = Q - NQ if FIN == 0 else Q + M
     ops = []
     hist = {}
+    at = [-1, 0]
 
     def op(q, ck, fn, reads=(), writes=(), sem=None, deps=(), kind="c", name=""):
         i = len(ops)
@@ -168,7 +134,7 @@ def build(g, T, topo, core, rank):
             hist[b] = [e for e in h if not (lo <= e[0] and e[1] <= hi)] + [(lo, hi, i, True)]
         for (b, lo, hi) in reads:
             hist.setdefault(b, []).append((lo, hi, i, False))
-        ops.append({"q": q, "ck": ck, "fn": fn, "deps": dd, "sem": sem, "kind": kind, "name": name})
+        ops.append({"q": q, "ck": ck, "fn": fn, "deps": dd, "sem": sem, "kind": kind, "name": name, "t": at[0], "j": at[1]})
         return i
 
     def V(n, fn, reads, writes, name=""):
@@ -177,234 +143,500 @@ def build(g, T, topo, core, rank):
     def S(n, fn, reads, writes, name="", deps=(), k="s"):
         return op("S", (k, n), fn, reads, writes, name=name, deps=deps)
 
-    def SG(n, fn, reads, writes, name=""):
-        return op("S", ("gather", n), fn, reads, writes, name=name)
+    def gather(q, out, win, lst, n, reads, writes, name):
+        if q == "S":
+            return op("S", ("gather", n), lambda: sc.activation(out, win.indirect(lst), F.Copy), reads, writes, name=name)
+        return op("V", ("gather", n), lambda: v.tensor_copy(out, win.indirect(lst)), reads, writes, name=name)
 
     def full(b):
         return (b, 0, 1 << 20)
 
     v, sc, te, sy = g.vector, g.scalar, g.tensor, g.sync
 
-    for b, c in (("fK", KE), ("fN", -KE), ("fP", KV), ("fQ", -KV), ("fE", 1.0), ("hP", -3.5 * KV), ("hQ", 3.5 * KV), ("f1", 1.0), ("fF", 1.0), ("mask", 1.0)):
-        V(512 if b == "mask" else 64, lambda b=b, c=c: v.memset(T[b][:], c), [], [full(b)], "fill")
-    V(64, lambda: v.memset(T.mask[:, 0::16], 0.0), [], [full("mask")], "mask")
-    for t in range(ST):
-        V(64, lambda t=t: v.memset(T["MS%d" % t][:, CW:CT], 0.0), [], [("MS%d" % t, CW, CT)], "MSpad")
+    fills = [("id1", 1.0), ("bP", KV), ("e3", 1.0), ("f1", 1.0), ("mask", 1.0), ("cu32", 0)] + [("mm%d" % h, 0.0) for h in range(len(parts))]
+    for b, c in fills:
+        V(SCRATCH[b][1][1] / 2, lambda b=b, c=c: v.memset(T[b][:], c), [], [full(b)], "fill")
+    V(64, lambda: v.memset(T.mask[:, 0::16], 0.0), [], [full("mask")], "fill")
+    V(64, lambda: v.memset(T.hb[:, 0:64], -3.5 * KV), [], [("hb", 0, 64)], "fill")
+    V(64, lambda: v.memset(T.hb[:, 64:128], 3.5 * KV), [], [("hb", 64, 128)], "fill")
 
     def sel(out, src, n, pattern, cmp, base, cm):
         op("G", ("sel", n), lambda: g.affine_select(T[out][:], T[src][:], pattern, cmp, 0.0, base, cm), [full(src)], [full(out)], name="sel")
 
-    op("G", ("us", 0.2), lambda: g.iota(T.pt[:], [[0, NQ]], 0, 1), [], [full("pt")], name="iota")
-    op("G", ("us", 0.2), lambda: g.iota(T.q16[:], [[16, NQ]], 0, 0), [], [full("q16")], name="iota")
-    for o, f in (("idN", "fN"), ("idK", "fK"), ("idF", "fF"), ("id1", "f1")):
-        sel(o, f, 128, [[-1, 128]], A.is_equal, 0, 1)
-    for x in "PQ":
-        sel("b" + x + "1", "f" + x, 128, [[-16, 8], [0, 16]], A.is_ge, 0, 1)
-        sel("b" + x, "b" + x + "1", 128, [[16, 8], [0, 16]], A.is_ge, 15, -1)
-    sel("e1", "fE", 144, [[0, 9], [1, 16]], A.is_equal, -15, 0)
-    sel("e2", "e1", 144, [[-16, 9], [0, 16]], A.is_ge, 0, 1)
-    sel("e3", "e2", 144, [[16, 9], [0, 16]], A.is_ge, 15, -1)
+    op("G", ("us", 0.2), lambda: g.iota(T.pt[:], [[0, 2 * Q]], 0, 1), [], [full("pt")], name="iota")
+    op("G", ("us", 0.2), lambda: g.iota(T.q16[:], [[16, 2 * Q]], 0, 0), [], [full("q16")], name="iota")
+    sel("id1", "id1", 128, [[-1, 128]], A.is_equal, 0, 1)
+    sel("bP", "bP", 128, [[-16, 8], [0, 16]], A.is_ge, 0, 1)
+    sel("bP", "bP", 128, [[16, 8], [0, 16]], A.is_ge, 15, -1)
+    sel("e3", "e3", 144, [[0, 9], [1, 16]], A.is_equal, -15, 0)
+    sel("e3", "e3", 144, [[-16, 9], [0, 16]], A.is_ge, 0, 1)
+    sel("e3", "e3", 144, [[16, 9], [0, 16]], A.is_ge, 15, -1)
+    scaled = [("idN", "id1", -KE), ("idK", "id1", KE), ("idF", "id1", 1.0), ("idW", "id1", -float(W)), ("idA", "id1", 16.0), ("idB", "id1", -16.0), ("bQ", "bP", -1.0)]
+    for o, f, c in scaled + [("idH%d" % h, "id1", -float(e - a)) for h, (j0, j1, a, e) in enumerate(parts)]:
+        V(128, lambda o=o, f=f, c=c: v.tensor_scalar(T[o][:], T[f][:], c, None, A.mult), [full(f)], [full(o)], "k")
 
-    V(NQ, lambda: v.tensor_scalar(T.pa[:], T.pt[:], 15, None, A.bitwise_and), [full("pt")], [full("pa")])
-    V(NQ, lambda: v.tensor_tensor(T.cl[:], T.pa[:], T.q16[:], A.add), [full("pa"), full("q16")], [full("cl")])
-    V(NQ, lambda: v.tensor_scalar(T.c16[:], T.cl[:], 16.0, None, A.mult), [full("cl")], [full("c16")])
-    for t in range(ST - 1):
-        b = "TW%d" % t
-        V(NQ, lambda b=b: v.tensor_scalar(T[b][:, 18:32], T.cl[:], 1.0, None, A.mult), [full("cl")], [(b, 18, 32)])
+    V(NQ, lambda: v.tensor_scalar(T.pa[:], T.pt[:], 15, None, A.bitwise_and), [full("pt")], [full("pa")], "k")
+    V(NQ, lambda: v.tensor_tensor(T.cl[:], T.pa[:], T.q16[:], A.add), [full("pa"), full("q16")], [full("cl")], "k")
+    V(NQ, lambda: v.tensor_scalar(T.c16[:], T.cl[:], 16.0, None, A.mult), [full("cl")], [full("c16")], "k")
+    for h, (j0, j1, a, e) in enumerate(parts):
+        n, q0, cb = e - a, a // 16, T["cb%d" % h]
+        CB = "cb%d" % h
+        V(NQ, lambda cb=cb, q0=q0: v.tensor_copy(cb[:, 0:Q], T.cl[:, q0:q0 + Q]), [full("cl")], [(CB, 0, Q)], "k")
+        V(NQ, lambda cb=cb, n=n: v.tensor_scalar(cb[:, Q:2 * Q], T.cl[:, 0:Q], float(n), None, A.add), [full("cl")], [(CB, Q, 2 * Q)], "k")
+        V(NQ, lambda cb=cb: v.memset(cb[:, 2 * Q:3 * Q], float(W)), [], [(CB, 2 * Q, 3 * Q)], "k")
+        for t in range(ST - 1):
+            b = "TW%d_%d" % (t, h)
+            V(NQ, lambda b=b, n=n, cb=cb: v.tensor_copy(T[b][:, 2 * n + 2 * Q:2 * n + 4 * Q], cb[:, Q:3 * Q]), [full(CB)], [(b, 2 * n + 2 * Q, 2 * n + 4 * Q)], "k")
 
-    dq = {"Y": sy, "S": sc}
     nld = [0]
     amount = [0]
-    prev = {"Y": [], "S": []}
+    prev = []
 
-    def load(q, out, in_, b, lo, hi):
+    def load(out, in_, b, lo, hi):
         k = nld[0]
         nld[0] += 1
         amount[0] += hi - lo
-        i = op(q, ("us", 0.06), lambda: dq[q].dma_start(out, in_), [], [], sem="ld%d" % k, kind="dma", name="ld", deps=prev[q])
-        prev[q] = [i]
+        i = op("Y", ("us", 0.06), lambda: sy.dma_start(out, in_), [], [(b, lo, hi)], sem="ld%d" % k, kind="dma", name="ld", deps=prev[-1:])
+        prev.append(i)
         op("X", ("ld", amount[0] / 896.0), None, [], [(b, lo, hi)], sem=("ld%d" % k, 16), kind="arr", deps=[i], name="land")
 
-    def load_c(q, p):
-        lo, hi = CP[p]
-        load(q, T.ck32[:, lo:hi], T.ck[:, lo:hi], "ck32", lo, hi)
+    load(T.cuin[:], T.cu[:], "cuin", 0, NQ)
+    V(NQ, lambda: v.tensor_copy(T.cu32[:, 0:NQ], T.cuin[:]), [full("cuin")], [full("cu32")], "k")
+    load(T.gap32[:], T.gap[:], "gap32", 0, M)
+    lead = PAR["lead"]
+    for src, (lo, hi) in [("ck", x) for x in CP[:lead]] + [("la", x) for x in LP] + [("ck", x) for x in CP[lead:]]:
+        load(T[src + "32"][:, lo:hi], T[src][:, lo:hi], src + "32", lo, hi)
 
-    def load_l(q, p):
-        lo, hi = LP[p]
-        load(q, T.la32[:, lo:hi], T.la[:, lo:hi], "la32", lo, hi)
+    for h, (j0, j1, a, e) in enumerate(parts):
+        n, q0, b = e - a, a // 16, "TW0_%d" % h
+        for k in range(2):
+            V(NQ, lambda b=b, n=n, q0=q0, k=k: v.tensor_scalar(T[b][:, 2 * n + k * Q:2 * n + k * Q + Q], T.cu32[:, q0:q0 + Q], float(k), None, A.add),
+              [full("cu32")], [(b, 2 * n + k * Q, 2 * n + k * Q + Q)], "k")
+    V(NQ, lambda: v.tensor_tensor(T.il32[:, 0:Q], T.cu32[:, 0:Q], T.c16[:, 0:Q], A.add), [full("cu32"), full("c16")], [full("il32")], "il")
+    V(NQ, lambda: v.tensor_copy(T.il[:, 0:NQ], T.il32[:, 0:NQ]), [full("il32")], [("il", 0, Q)], "il")
+    V(NQ, lambda: v.tensor_copy(T.il[:, Q + 1:Q + 1 + NQ], T.il32[:, 0:NQ]), [full("il32")], [("il", Q, 2 * Q)], "il")
 
-    load("Y", T.cu32[:], T.cu[:], "cu32", 0, NQ)
-    load("Y", T.gap32[:], T.gap[:], "gap32", 0, M)
-    load_c("Y", 0)
-    for p in range(len(LP)):
-        load_l("Y", p)
-    for p in range(1, len(CP)):
-        load_c("Y", p)
+    def first(a, e):
+        o = (Q + 1) * (a // 16 % 2)
+        return T.il[:, o + a // 16:o + e // 16]
 
-    V(NQ, lambda: v.tensor_copy(T.TW0[:, CW:CW + NQ], T.cu32[:]), [full("cu32")], [("TW0", CW, CW + NQ)])
-    V(NQ, lambda: v.tensor_tensor(T.il32[:], T.cu32[:], T.c16[:], A.add), [full("cu32"), full("c16")], [full("il32")])
-    V(NQ, lambda: v.tensor_copy(T.il[:], T.il32[:]), [full("il32")], [full("il")])
-    for a, e in CHUNKS:
-        op("V", ("gather", e - a), lambda a=a, e=e: v.tensor_copy(T.Iu[:, a:e], T.ck32[:, 0:16 * e].indirect(T.il[:, a // 16:e // 16])),
-           [("ck32", 0, 16 * e), full("il")], [("Iu", a, e)], name="Iu0")
+    for j, (a, e) in enumerate(chunks):
+        at[1] = j
+        gather("V", T.Iu[:, a:e], T.ck32[:, 0:16 * e], first(a, e), e - a, [("ck32", 0, 16 * e), full("il")], [("Iu", a, e)], "Iu0")
     exps = []
 
-    def encode(src, f, o, lo, hi, q, k="s"):
+    def encode(src, f, o, lo, hi, q):
         if q == "V":
             V(hi - lo, lambda: v.tensor_copy(T[f][:, lo:hi], T[src][:, lo:hi]), [(src, lo, hi)], [(f, lo, hi)], "conv")
         else:
-            op("G", ("sel", hi - lo), lambda: g.affine_select(T[f][:, lo:hi], T[src][:, lo:hi], [[0, hi - lo]], A.is_ge, 0.0, 0, 0), [(src, lo, hi)], [(f, lo, hi)], name="convg")
-        exps.append(S(hi - lo, lambda: sc.activation(T[o][:, lo:hi], T[f][:, lo:hi], F.Exp, bias=B0, scale=1.0 / SC), [(f, lo, hi)], [(o, lo, hi)], name="exp", k=k))
+            op("G", ("sel", hi - lo), lambda: g.affine_select(T[f][:, lo:hi], T[src][:, lo:hi], [[0, hi - lo]], A.is_ge, 0.0, 0, 0), [(src, lo, hi)], [(f, lo, hi)], name="conv")
+        exps.append(S(hi - lo, lambda: sc.activation(T[o][:, lo:hi], T[f][:, lo:hi], F.Exp, bias=B0, scale=1.0 / SC), [(f, lo, hi)], [(o, lo, hi)], name="exp"))
 
-    encode("ck32", "cf", "Cc", CP[0][0], CP[0][1], "V")
-    for lo, hi in LP:
-        encode("la32", "lf", "Lc", lo, hi, "V")
-    for lo, hi in CP[1:]:
-        encode("ck32", "cf", "Cc", lo, hi, "G")
-    V(M, lambda: v.tensor_scalar(T.gapf[:], T.gap32[:], 0.5, None, A.subtract), [full("gap32")], [full("gapf")])
+    V(M, lambda: v.tensor_scalar(T.gapf[:], T.gap32[:], 0.5, None, A.subtract), [full("gap32")], [full("gapf")], "gapf")
     exps.append(S(M, lambda: sc.activation(T.gc0[:], T.gapf[:], F.Exp, scale=1.0 / SC), [full("gapf")], [full("gc0")], name="expg", k="stab"))
+    for k, (lo, hi) in enumerate(LP):
+        at[1] = 10 + k
+        encode("la32", "lf", "Lc", lo, hi, "V")
+    for j, (a, e) in enumerate(cuts(PAR["cp"])):
+        at[1] = j
+        encode("ck32", "cf", "Cc", 16 * a, 16 * e, PAR["convc"][j])
 
     nloc = [0]
     cores = list(T.cores)
     nxt = cores[(rank + 1) % len(cores)]
+    ne = len(topo.engines(core, nxt))
 
     def send_gap():
         dst = [cores[(rank + d) % len(cores)] for d in (1, 2)]
         eng = [e for e in topo.engines(core, dst[0]) if e in topo.engines(core, dst[1])]
-        m = 0
-        for e in eng:
-            m |= 1 << e
-        ids = []
-        for d in dst:
-            a = topo.addr(d)
-            ids.append(DstId(rid=a[0], pnc=a[1]))
+        ids = [DstId(rid=topo.addr(d)[0], pnc=topo.addr(d)[1]) for d in dst]
         nloc[0] += len(eng)
-        g.remote_dma_fused([RemoteDMATransfer(dst_ids=ids, dma_engine_mask=m, remote_sem=T.sem.gap, srcs=[T.gc0[:]], dsts=[T.gc1[:], T.gc2[:]])], local_sem=T.sem.loc)
+        g.remote_dma_fused([RemoteDMATransfer(dst_ids=ids, dma_engine_mask=sum(1 << e for e in eng), remote_sem=T.sem.gap, srcs=[T.gc0[:]], dsts=[T.gc1[:], T.gc2[:]])], local_sem=T.sem.loc)
 
     i = op("G", ("send", 1), send_gap, [full("gc0")], [], kind="send", name="gap")
-    ne = len(topo.engines(core, nxt))
     op("X", ("us", 5.0), None, [], [full("gc1"), full("gc2")], sem=("gap", 2 * ne), kind="arr", deps=[i], name="agap")
 
-    def send(out, in_, sem):
-        a = topo.addr(nxt)
-        nloc[0] += ne
-        g.remote_dma(out, in_, T.sem[sem], T.sem.loc, a[1], a[0], topo.mask(core, nxt))
+    def send(name, sem, dst, lo, hi, srcs):
+        def fn():
+            a = topo.addr(nxt)
+            nloc[0] += ne
+            if len(srcs) == 1:
+                b, c = srcs[0]
+                g.remote_dma(T[dst][:, lo:hi], T[b][:, c:c + hi - lo], T.sem[sem], T.sem.loc, a[1], a[0], topo.mask(core, nxt))
+            else:
+                g.remote_dma_fused([RemoteDMATransfer(dst_ids=[DstId(rid=a[0], pnc=a[1])], dma_engine_mask=topo.mask(core, nxt), remote_sem=T.sem[sem],
+                                                      srcs=[T[b][:, c:c + hi - lo] for b, c in srcs], dsts=[T[dst][:, lo:hi]], alu_op=2)], local_sem=T.sem.loc)
+        i = op("G", ("send", 1), fn, [(b, c, c + hi - lo) for b, c in srcs], [], kind="send", name=name)
+        op("X", ("net", 1), None, [], [(dst, lo, hi)], sem=(sem, ne), kind="arr", deps=[i], name="arr" + name)
 
-    cn = "ps%d" % CB
-    pc = T[cn]
-    SG(M, lambda: sc.activation(T.Ic0[:], T.Cc[:, 0:W].indirect(T.il[:]), F.Copy), [("Cc", 0, W), full("il")], [full("Ic0")], name="Ic0")
+    gn, cn = "ps6", "ps7"
+    pg, pc = T[gn], T[cn]
 
-    def step(t):
-        last = t == ST - 1
-        IC, TW, MS, IP = "Ic%d" % t, "TW%d" % t, "MS%d" % t, "IP%d" % t
-        Icb, TWb, MSb, IPb = T[IC], T[TW], T[MS], T[IP]
-        if not last:
-            gb = "gc%d" % t
-            op("P", ("mm", 14), lambda: te.matmul(pc[:, 16:240], T.idF[:], T[gb][:], True, True), [full("idF"), full(gb)], [full(cn)], name="gapc")
-            if t == 0:
-                V(M, lambda: v.tensor_tensor(TWb[:, CT:CR], T.Ic0[:], pc[:, 16:240], A.mult), [full("Ic0"), full(cn)], [("TW0", CT, CR)], "Tc0")
-        for j, (a, e) in enumerate(CHUNKS):
-            n = e - a
-            xb, yb, Pb, ub = T["x%d" % j], T["y%d" % j], T["P%d" % j], T["u%d" % j]
-            X, Y, P, U = "x%d" % j, "y%d" % j, "P%d" % j, "u%d" % j
-            if t > 0:
-                S(n, lambda a=a, e=e: sc.activation(T.lnI[:, a:e], Icb[:, a:e], F.Ln, scale=UP), [(IC, a, e)], [("lnI", a, e)], name="lnI%d" % j)
-                V(n, lambda a=a, e=e: v.tensor_scalar(T.Iu[:, a:e], T.lnI[:, a:e], SC, OFF + 0.25, A.mult, A.add), [("lnI", a, e)], [("Iu", a, e)], "decI%d" % j)
-            SG(16 * n, lambda a=a, e=e, xb=xb: sc.activation(xb[:], T.Lc[:].indirect(T.Iu[:, a:e]), F.Copy), [full("Lc"), ("Iu", a, e)], [full(X)], name="G1_%d" % j)
-            V(8 * n, lambda n=n, xb=xb, Pb=Pb: v.tensor_tensor_scan(Pb[:], T.mask[:, 0:16 * n], xb[:], 0.0, A.mult, A.max), [full("mask"), full(X)], [full(P)], "scan1_%d" % j)
-            bk = BANKS[j]
-            per = 16 // len(bk)
-            for h, b in enumerate(bk):
-                def diff(n=n, xb=xb, Pb=Pb, h=h, k=len(bk), per=per, pb=T["ps%d" % b]):
-                    te.matmul(pb[:, 0:per * n], T.idN[:], xb[:, h::k], True, False)
-                    for i in range(per):
-                        r = te.matmul(pb[:, i:per * n:per], T.idK[:], Pb[:, 15::16], False, i == per - 1)
-                    return r
+    def first_acquires(t, j):
+        a, e = chunks[j]
+        n = e - a
+        at[:] = [t, j]
+        IC = "Ic%d" % t
+        xb, yb, Pb, ub = T["x%d" % j], T["y%d" % j], T["P%d" % j], T["u%d" % j]
+        X, Y, P, U = "x%d" % j, "y%d" % j, "P%d" % j, "u%d" % j
+        if t > 0:
+            S(n, lambda: sc.activation(T.lnI[:, a:e], T[IC][:, a:e], F.Ln, scale=UP), [(IC, a, e)], [("lnI", a, e)], name="lnI")
+            V(n, lambda: v.tensor_scalar(T.Iu[:, a:e], T.lnI[:, a:e], SC, OFF + 0.25, A.mult, A.add), [("lnI", a, e)], [("Iu", a, e)], "decI")
+        gather("V" if t == 0 and j in PAR["g1v"] else "S", xb[:], T.Lc[:], T.Iu[:, a:e], 16 * n, [full("Lc"), ("Iu", a, e)], [full(X)], "G1")
+        V(8 * n, lambda: v.tensor_tensor_scan(Pb[:], T.mask[:, 0:16 * n], xb[:], 0.0, A.mult, A.max), [full("mask"), full(X)], [full(P)], "scan1")
+        k = -(-n * 16 // 512)
+        per = 16 // k
+        for h in range(k):
+            b = "ps%d" % (2 * (j % 2) + h)
 
-                op("P", ("mm", per + per * n / 64), diff, [full("idK"), full("idN"), full(P), full(X)], [full("ps%d" % b)], name="diff%d_%d" % (j, h))
-                V(per * n, lambda n=n, xb=xb, yb=yb, h=h, k=len(bk), per=per, pb=T["ps%d" % b]: v.tensor_tensor(yb[:, h::k], xb[:, h::k], pb[:, 0:per * n], A.min),
-                  [full(X), full("ps%d" % b)], [(Y, h, h + 1)], "min%d_%d" % (j, h))
-            V(8 * n, lambda n=n, yb=yb, ub=ub: v.tensor_tensor_scan(ub[:], T.mask[:, 0:16 * n], yb[:], 0.0, A.mult, A.max), [full("mask"), full(Y)], [full(U)], "scan2_%d" % j)
-            S(n, lambda a=a, e=e, ub=ub: sc.activation(T.lnS[:, a:e], ub[:, 15::16], F.Ln, bias=EPS, scale=UP), [full(U)], [("lnS", a, e)],
-              deps=exps if t == 0 else (), name="lnS%d" % j, k="stab" if t == 0 and j == 0 else "s")
-            V(n, lambda a=a, e=e: v.tensor_scalar(T.su[:, a:e], T.lnS[:, a:e], SC, OFF + 0.25, A.mult, A.add), [("lnS", a, e)], [("su", a, e)], "decS%d" % j)
-        V(NQ, lambda: v.tensor_copy(T.ni[:, 0:14], TWb[:, CW:CW + NQ]), [(TW, CW, CW + NQ)], [("ni", 0, 14)], "n0")
-        V(NQ, lambda: v.tensor_scalar(T.ni[:, 14:28], TWb[:, CW:CW + NQ], 1.0, None, A.add), [(TW, CW, CW + NQ)], [("ni", 14, 28)], "n1")
-        V(NQ, lambda: v.tensor_scalar(T.nw[:], T.ni[:], 15, None, A.bitwise_and), [full("ni")], [full("nw")], "n2")
-        V(NQ, lambda: v.tensor_tensor(T.rl32[:], T.nw[:, 14:28], T.c16[:], A.add), [full("nw"), full("c16")], [full("rl32")], "n3")
-        V(NQ, lambda: v.tensor_copy(T.rl[:], T.rl32[:]), [full("rl32")], [full("rl")], "n4")
-        if not last:
-            V(NQ, lambda: v.tensor_tensor(TWb[:, 4:18], T.nw[:, 0:14], T.c16[:], A.add), [full("nw"), full("c16")], [(TW, 4, 18)], "n5")
-        SG(M, lambda: sc.activation(T.Rld[:], T.Cc[:, 0:W].indirect(T.rl[:]), F.Copy), [("Cc", 0, W), full("rl")], [full("Rld")], name="Rld")
-        if not last:
-            V(M, lambda: v.tensor_tensor(TWb[:, CR:CE], T.Rld[:], pc[:, 16:240], A.mult), [full("Rld"), full(cn)], [(TW, CR, CE)], "Tr")
-        for j, (a, e) in enumerate(CHUNKS):
-            n = e - a
-            zb, qb = T["z%d" % j], T["q%d" % j]
-            Z, Q = "z%d" % j, "q%d" % j
-            pn, qn = "ps%d" % BANKS[j][0], "ps%d" % BANKS[j][-1]
-            pb, qp = T[pn], T[qn]
+            op("P", ("mm", per * n), lambda h=h, pb=T[b]: te.matmul(pb[:, 0:per * n], T.idN[:], xb[:, h::k], True, False), [full("idN"), full(X)], [full(b)], name="neg%d" % h)
 
-            def prep(a=a, e=e, n=n, qp=qp):
-                te.matmul(qp[:, 256:256 + n], T.id1[:], Icb[:, a:e], True, True)
-                return te.matmul(qp[:, 320:320 + n], T.idF[:], TWb[:, CT + a:CT + e], True, True)
-
-            op("P", ("mm", 5), prep, [full("id1"), full("idF"), (IC, a, e), (TW, CT + a, CT + e)], [full(qn)], name="prep%d" % j)
-            SG(16 * n, lambda a=a, e=e, zb=zb: sc.activation(zb[:], T.Cc[:, 0:W].indirect(T.su[:, a:e]), F.Copy), [("Cc", 0, W), ("su", a, e)], [full(Z)], name="G2_%d" % j)
-            V(8 * n, lambda n=n, zb=zb, qb=qb: v.tensor_tensor_scan(qb[:], T.mask[:, 0:16 * n], zb[:], 0.0, A.mult, A.max), [full("mask"), full(Z)], [full(Q)], "scan3_%d" % j)
-            V(n, lambda a=a, e=e, n=n, qb=qb, qp=qp: v.tensor_tensor(T.Inew[:, a:e], qb[:, 15::16], qp[:, 256:256 + n], A.max), [full(qn), full(Q)], [("Inew", a, e)], "Inew%d" % j)
-            V(n, lambda a=a, e=e, n=n, qp=qp: v.tensor_tensor(T.R[:, a:e], T.Inew[:, a:e], qp[:, 320:320 + n], A.is_ge), [("Inew", a, e), full(qn)], [("R", a, e)], "R%d" % j)
-
-            def votes(a=a, e=e, n=n, pb=pb):
-                for k, (w, h) in enumerate((("bP", "hP"), ("bQ", "hQ"))):
-                    o = pb[:, k * n:k * n + n]
-                    te.matmul(o, T[w][:], T.R[:, a:e], True, False)
-                    r = te.matmul(o, T[h][0:1, :], T.f1[0:1, 0:n], False, True)
+            def diff(h=h, pb=T[b]):
+                for i in range(per):
+                    r = te.matmul(pb[:, i:per * n:per], T.idK[:], Pb[:, 15::16], False, i == per - 1)
                 return r
 
-            op("P", ("mm", 4), votes, [full("bP"), full("bQ"), full("hP"), full("hQ"), full("f1"), ("R", a, e)], [full(pn)], name="vote%d" % j)
-            V(n, lambda a=a, e=e, n=n, pb=pb: v.tensor_tensor(T.s2[:, a:e], T.Inew[:, a:e], pb[:, n:2 * n], A.min), [("Inew", a, e), full(pn)], [("s2", a, e)], "s2_%d" % j)
-            V(n, lambda a=a, e=e, n=n, pb=pb: v.tensor_tensor(pb[:, 128:128 + n], T.Rld[:, a:e], pb[:, 0:n], A.min), [("Rld", a, e), full(pn)], [full(pn)], "s1_%d" % j)
-            V(n, lambda a=a, e=e, n=n, pb=pb: v.tensor_tensor(IPb[:, a:e], T.s2[:, a:e], pb[:, 128:128 + n], A.max), [full(pn), ("s2", a, e)], [(IP, a, e)], "IP%d" % j)
-            nm = "a%d_%d" % (t, j)
-            i = op("G", ("send", 1), lambda a=a, e=e, nm=nm: send(T["Ic%d" % (t + 1)][:, a:e], IPb[:, a:e], nm), [(IP, a, e)], [], kind="send", name="A%d" % j)
-            op("X", ("net", 1), None, [], [("Ic%d" % (t + 1), a, e)], sem=(nm, ne), kind="arr", deps=[i], name="arrA%d" % j)
+            op("P", ("mm", per * max(n, 64)), diff, [full("idK"), full(P)], [full(b)], name="diff%d" % h)
+            V(per * n, lambda h=h, pb=T[b]: v.tensor_tensor(yb[:, h::k], xb[:, h::k], pb[:, 0:per * n], A.min), [full(X), full(b)], [(Y, h, h + 1)], "min%d" % h)
+        V(8 * n, lambda: v.tensor_tensor_scan(ub[:], T.mask[:, 0:16 * n], yb[:], 0.0, A.mult, A.max), [full("mask"), full(Y)], [full(U)], "scan2")
+        S(n, lambda: sc.activation(T.lnS[:, a:e], ub[:, 15::16], F.Ln, bias=EPS, scale=UP), [full(U)], [("lnS", a, e)],
+          deps=exps if t == 0 else (), name="lnS", k="stab" if t == 0 and j == 0 else "s")
+        V(n, lambda: v.tensor_scalar(T.su[:, a:e], T.lnS[:, a:e], SC, OFF + 0.25, A.mult, A.add), [("lnS", a, e)], [("su", a, e)], "decS")
+
+    def reloads(t, h):
+        j0, j1, a, e = parts[h]
+        at[:] = [t, j0]
+        last = t == ST - 1
+        n, nq = e - a, (e - a) // 16
+        TW, NW, RL = "TW%d_%d" % (t, h), "nw%d" % h, "rl%d" % h
+        tw, c = T[TW], 2 * n
+        if t == 0:
+            gather(PAR["zq"][0], T.Ic0[:, a:e], T.Cc[:, 0:16 * e], first(a, e), n, [("Cc", 0, 16 * e), full("il")], [("Ic0", a, e)], "Ic0")
+        if not last:
+            gb = "gc%d" % t
+            op("P", ("mm", 4 * n), lambda: te.matmul(pg[:, a:e], T.idF[:], T[gb][:, a:e], True, True), [full("idF"), full(gb)], [full(gn)], name="gapc")
+            if t == 0:
+                V(n, lambda: v.tensor_tensor(tw[:, n:c], T.Ic0[:, a:e], pg[:, a:e], A.mult), [("Ic0", a, e), full(gn)], [(TW, n, c)], "Tc0")
+        V(2 * Q, lambda: v.tensor_scalar(T[NW][:], tw[:, c:c + 2 * Q], 15.5, None, A.is_ge), [(TW, c, c + 2 * Q)], [full(NW)], "n0")
+
+        def column():
+            te.matmul(pc[:, 128:128 + Q], T.id1[:], tw[:, c + Q:c + 2 * Q], True, False)
+            te.matmul(pc[:, 128:128 + Q], T.idA[:], T["cb%d" % h][:, 0:Q], False, False)
+            return te.matmul(pc[:, 128:128 + Q], T.idB[:], T[NW][:, Q:2 * Q], False, True)
+
+        op("P", ("mm", 192), column, [full("id1"), full("idA"), full("idB"), full("cb%d" % h), full(NW), (TW, c, c + 2 * Q)], [full(cn)], name="col")
+        V(Q, lambda: v.tensor_copy(T[RL][:], pc[:, 128:128 + Q]), [full(cn)], [full(RL)], "n1")
+        gather(PAR["zq"][1] if t == 0 else PAR["rq"], T.Rld[:, a:e], T.Cc[:, 0:W], T[RL][:, 0:nq], n, [("Cc", 0, W), full(RL)], [("Rld", a, e)], "Rld")
+        if not last:
+            V(n, lambda: v.tensor_tensor(tw[:, 0:n], T.Rld[:, a:e], pg[:, a:e], A.mult), [("Rld", a, e), full(gn)], [(TW, 0, n)], "Tr")
+        else:
+            S(n, lambda: sc.activation(T.lnR[:, a:e], T.Rld[:, a:e], F.Ln, scale=UP), [("Rld", a, e)], [("lnR", a, e)], name="lnR")
+            V(n, lambda: v.tensor_scalar(T.Ri[:, a:e], T.lnR[:, a:e], SC, OFF, A.mult, A.add), [("lnR", a, e)], [("Ri", a, e)], "decR")
+
+    def join(t, j):
+        a, e = chunks[j]
+        n = e - a
+        at[:] = [t, j]
+        last = t == ST - 1
+        h = [k for k, p in enumerate(parts) if p[0] <= j < p[1]][0]
+        TW, c = "TW%d_%d" % (t, h), parts[h][3] - 2 * parts[h][2]
+        IC, Z, QB, pn = "Ic%d" % t, "z%d" % j, "q%d" % j, "ps%d" % (4 + j % 2)
+        zb, qb, pb = T[Z], T[QB], T[pn]
+
+        def prep():
+            te.matmul(pb[:, 256:256 + n], T.id1[:], T[IC][:, a:e], True, True)
+            te.matmul(pb[:, 320:320 + n], T.id1[:], T[TW][:, c + a:c + e], True, True)
+            return te.matmul(pb[:, 0:128], T.f1[0:1, :], T.hb[0:1, :], True, False)
+
+        op("P", ("mm", 256), prep, [full("id1"), full("f1"), full("hb"), (IC, a, e), (TW, c + a, c + e)], [full(pn)], name="prep")
+        gather("V" if t == 0 and j in PAR["g2v"] else "S", zb[:], T.Cc[:, 0:W], T.su[:, a:e], 16 * n, [("Cc", 0, W), ("su", a, e)], [full(Z)], "G2")
+        V(8 * n, lambda: v.tensor_tensor_scan(qb[:], T.mask[:, 0:16 * n], zb[:], 0.0, A.mult, A.max), [full("mask"), full(Z)], [full(QB)], "scan3")
+        V(n, lambda: v.tensor_tensor(T.Inew[:, a:e], qb[:, 15::16], pb[:, 256:256 + n], A.max), [full(pn), full(QB)], [("Inew", a, e)], "Inew")
+        V(n, lambda: v.tensor_tensor(T.R[:, a:e], T.Inew[:, a:e], pb[:, 320:320 + n], A.is_ge), [("Inew", a, e), full(pn)], [("R", a, e)], "R")
+
+        def votes():
+            te.matmul(pb[:, 0:n], T.bP[:], T.R[:, a:e], False, False)
+            return te.matmul(pb[:, 64:64 + n], T.bQ[:], T.R[:, a:e], False, True)
+
+        op("P", ("mm", 128), votes, [full("bP"), full("bQ"), ("R", a, e)], [full(pn)], name="vote")
+        if last:
+            S(n, lambda: sc.activation(T.lnI[:, a:e], T.Inew[:, a:e], F.Ln, scale=UP), [("Inew", a, e)], [("lnI", a, e)], name="lnN")
+            V(n, lambda: v.tensor_scalar(T.Ni[:, a:e], T.lnI[:, a:e], SC, OFF, A.mult, A.add), [("lnI", a, e)], [("Ni", a, e)], "decN")
+            new, rld, s2, out, dst = "Ni", "Ri", "f2s", "fo", "fi"
+        else:
+            new, rld, s2, out, dst = "Inew", "Rld", "s2%d" % t, "IP%d" % t, "Ic%d" % (t + 1)
+        V(n, lambda: v.tensor_tensor(T[s2][:, a:e], T[new][:, a:e], pb[:, 64:64 + n], A.min), [(new, a, e), full(pn)], [(s2, a, e)], "s2")
+        if PAR["fold"] and not last:
+            V(n, lambda: v.tensor_tensor(T[out][:, a:e], T[rld][:, a:e], pb[:, 0:n], A.min), [(rld, a, e), full(pn)], [(out, a, e)], "s1")
+            send("A", "a%d_%d" % (t, j), dst, a, e, [(out, a), (s2, a)])
+            return
+        V(n, lambda: v.tensor_tensor(pb[:, 128:128 + n], T[rld][:, a:e], pb[:, 0:n], A.min), [(rld, a, e), full(pn)], [full(pn)], "s1")
+        o = Q if last else 0
+        V(n, lambda: v.tensor_tensor(T[out][:, o + a:o + e], T[s2][:, a:e], pb[:, 128:128 + n], A.max), [full(pn), (s2, a, e)], [(out, o + a, o + e)], "IP")
+        if not (last and j == FIN):
+            send("A", "a%d_%d" % (t, j), dst, o + a, o + e, [(out, o + a)])
+
+    def lists(t, h):
+        j0, j1, a, e = parts[h]
+        at[:] = [t, j1 - 1]
+        last = t == ST - 1
+        n, nq = e - a, (e - a) // 16
+        TW, MS, LS, MM, NI, NW = "TW%d_%d" % (t, h), "MS%d_%d" % (t, h), "ls%d" % h, "mm%d" % h, "ni%d" % h, "nw%d" % h
+        tw, c = T[TW], 2 * n
 
         def count():
             for p in range(16):
-                r = te.matmul(pc[:, 0:NQ], T.e3[:, 15 - p:143 - p], T.R[:, p::16], p == 0, p == 15)
+                r = te.matmul(pg[:, 256:256 + nq], T.e3[:, 15 - p:143 - p], T.R[:, a + p:e:16], p == 0, p == 15)
             return r
 
-        op("P", ("mm", 16), count, [full("e3"), full("R")], [full(cn)], name="count")
-        lo = 28 if last else 0
-        if not last:
-            V(NQ, lambda: v.tensor_scalar(T.pm[:, 0:14], pc[:, 0:NQ], 3.5, float(W), A.is_lt, A.mult), [full(cn)], [("pm", 0, 14)], "c0")
-            V(NQ, lambda: v.tensor_scalar(T.pm[:, 14:28], pc[:, 0:NQ], 3.5, float(M), A.is_ge, A.mult), [full(cn)], [("pm", 14, 28)], "c1")
-        V(NQ, lambda: v.tensor_scalar(T.pm[:, 28:42], pc[:, 0:NQ], 3.5, None, A.is_ge), [full(cn)], [("pm", 28, 42)], "c2")
-        V(42, lambda: v.tensor_tensor(MSb[:, 4 + lo:46], T.pm[:, lo:42], TWb[:, 4 + lo:46], A.add), [("pm", lo, 42), (TW, 4 + lo, 46)], [(MS, 4 + lo, 46)], "c3")
-        if not last:
-            V(28, lambda: v.tensor_copy(T.lst[:], MSb[:, 4:32]), [(MS, 4, 32)], [full("lst")], "c4")
-            SG(M, lambda: sc.activation(MSb[:, CT:CR], TWb[:, CT:CE].indirect(T.lst[:, 14:28]), F.Copy), [(TW, CT, CE), full("lst")], [(MS, CT, CR)], name="Tsel")
-            op("V", ("scatter", M), lambda: v.tensor_copy(T.Cc[:].indirect(T.lst[:, 0:14]), T.Inew[:]), [full("Inew"), full("lst")], [full("Cc")], name="scatter")
-        hi = CT if last else CR
-        i = op("G", ("send", 1), lambda: send(T["TW%d" % (t + 1)][:, CW:hi], MSb[:, CW:hi], "b%d" % t), [(MS, CW, hi)], [], kind="send", name="B")
-        op("X", ("net", 1), None, [], [("TW%d" % (t + 1), CW, hi)], sem=("b%d" % t, ne), kind="arr", deps=[i], name="arrB")
+        op("P", ("mm", 1024), count, [full("e3"), ("R", a, e)], [full(gn)], name="count")
+        V(Q, lambda: v.tensor_scalar(T[MM][:, 0:nq], pg[:, 256:256 + nq], 3.5, None, A.is_ge), [full(gn)], [full(MM)], "c0")
+        if last:
+            op("P", ("mm", 64), lambda: te.matmul(pc[:, 0:Q], T.id1[:], tw[:, c:c + Q], True, False), [full("id1"), (TW, c, c + Q)], [full(cn)], name="base")
+            op("P", ("mm", 64), lambda: te.matmul(pc[:, 0:Q], T.id1[:], T[MM][:], False, True), [full("id1"), full(MM)], [full(cn)], name="spread")
+            V(Q, lambda: v.tensor_scalar(T[NI][:], pc[:, 0:Q], 15.5, -16.0, A.is_ge, A.mult), [full(cn)], [full(NI)], "c1")
+            V(Q, lambda: v.tensor_tensor(T.fo[:, YC + a // 16:YC + e // 16], T[NI][:, 0:nq], pc[:, 0:nq], A.add), [full(NI), full(cn)], [("fo", YC + a // 16, YC + e // 16)], "c2")
+            return
+
+        def base():
+            te.matmul(pc[:, 0:4 * Q], T.id1[:], tw[:, c:c + 4 * Q], True, False)
+            te.matmul(pc[:, 3 * Q:4 * Q], T.id1[:], tw[:, c:c + Q], False, False)
+            te.matmul(pc[:, 3 * Q:4 * Q], T.idA[:], T["cb%d" % h][:, 0:Q], False, False)
+            return te.matmul(pc[:, 3 * Q:4 * Q], T.idB[:], T[NW][:, 0:Q], False, False)
+
+        def spread():
+            for k, w in enumerate(("id1", "id1", "idH%d" % h, "idW")):
+                r = te.matmul(pc[:, k * Q:k * Q + Q], T[w][:], T[MM][:], False, k == 3)
+            return r
+
+        op("P", ("mm", 256), base, [full("id1"), full("idA"), full("idB"), full("cb%d" % h), full(NW), (TW, c, c + 4 * Q)], [full(cn)], name="base")
+        op("P", ("mm", 256), spread, [full("id1"), full("idW"), full("idH%d" % h), full(MM)], [full(cn)], name="spread")
+        ms = T[MS]
+        V(2 * Q, lambda: v.tensor_copy(T[LS][:], pc[:, 2 * Q:4 * Q]), [full(cn)], [full(LS)], "c2")
+        if PAR["uq"] == "S":
+            S(2 * Q, lambda: sc.activation(ms[:, n:n + 2 * Q], pc[:, 0:2 * Q], F.Copy), [], [full(cn), (MS, n, n + 2 * Q)], name="c1")
+        else:
+            V(2 * Q, lambda: v.tensor_copy(ms[:, n:n + 2 * Q], pc[:, 0:2 * Q]), [full(cn)], [(MS, n, n + 2 * Q)], "c1")
+        gather(PAR["tq"], ms[:, 0:n], tw[:, 0:c], T[LS][:, 0:nq], n, [(TW, 0, c), full(LS)], [(MS, 0, n)], "Tsel")
+        send("B", "b%d_%d" % (t, h), "TW%d_%d" % (t + 1, h), n, c + 2 * Q, [(MS, 0)])
+
+    def scatter(t, h):
+        j0, j1, a, e = parts[h]
+        at[:] = [t, j1 - 1]
+        LS = "ls%d" % h
+        op("V", ("scatter", e - a), lambda: v.tensor_copy(T.Cc[:].indirect(T[LS][:, Q:Q + (e - a) // 16]), T.Inew[:, a:e]), [("Inew", a, e), full(LS)], [full("Cc")], name="scatter")
 
     for t in range(ST):
-        step(t)
-    IC, TW = "Ic%d" % ST, "TW%d" % ST
-    Fb, Lb = T[IC], T[TW]
-    for j, (a, e) in enumerate(CHUNKS):
-        n = e - a
-        S(n, lambda a=a, e=e: sc.activation(T.lnI[:, a:e], Fb[:, a:e], F.Ln, scale=UP), [(IC, a, e)], [("lnI", a, e)], name="lnY")
-        V(n, lambda a=a, e=e: v.tensor_scalar(T.yint[:, a:e], T.lnI[:, a:e], SC, OFF, A.mult, A.add), [("lnI", a, e)], [("yint", a, e)])
-        V(n, lambda a=a, e=e: v.tensor_copy(T.yout[:, a:e], T.yint[:, a:e]), [("yint", a, e)], [("yout", a, e)])
-        op("Y", ("us", 0.1), lambda a=a, e=e: sy.dma_start(T.yi[:, a:e], T.yout[:, a:e]), [("yout", a, e)], [], sem="st%d" % j, kind="dma", name="yi")
-    V(NQ, lambda: v.tensor_copy(T.ni[:, 0:14], Lb[:, CW:CW + NQ]), [(TW, CW, CW + NQ)], [("ni", 0, 14)])
-    V(NQ, lambda: v.tensor_scalar(T.nw[:, 0:14], T.ni[:, 0:14], 15, None, A.bitwise_and), [("ni", 0, 14)], [("nw", 0, 14)])
-    V(NQ, lambda: v.tensor_copy(Lb[:, 4:18], T.nw[:, 0:14]), [("nw", 0, 14)], [(TW, 4, 18)])
-    op("Y", ("us", 0.1), lambda: sy.dma_start(T.yc[:], Lb[:, 4:18]), [(TW, 4, 18)], [], sem="st%d" % NC, kind="dma", name="yc")
+        for j in range(NC):
+            first_acquires(t, j)
+        for h in range(len(parts)):
+            reloads(t, h)
+        todo = list(range(NC)) if t < ST - 1 else [j for j in range(NC) if j != FIN] + [FIN]
+        for k, j in enumerate(todo):
+            join(t, j)
+            for h, (j0, j1, a, e) in enumerate(parts):
+                if j0 <= j < j1 and not [x for x in todo[k + 1:] if j0 <= x < j1]:
+                    lists(t, h)
+        if t < ST - 1:
+            for h in range(len(parts)):
+                scatter(t, h)
+    a, e = chunks[FIN]
+    at[:] = [ST - 1, FIN]
+    lo, hi = (Q - NQ, Q + e) if FIN == 0 else (Q + a, Q + M + NQ)
+    send("A", "a%d_%d" % (ST - 1, FIN), "fi", lo, hi, [("fo", lo)])
+    at[:] = [ST, 0]
+    for j, (a, e) in enumerate(chunks):
+        op("Y", ("us", 1.9), lambda a=a, e=e: sy.dma_start(T.yi[:, a:e], T.fi[:, Q + a:Q + e]), [("fi", Q + a, Q + e)], [], sem="st%d" % j, kind="dma", name="yi")
+    op("S", ("us", 1.9), lambda: sc.dma_start(T.yc[:], T.fi[:, YC:YC + NQ]), [("fi", YC, YC + NQ)], [], sem="st%d" % NC, kind="dma", name="yc")
     return ops, nloc
+
+
+PACE = [(1.05, 1.56, 0.42e-3, 0.08, 0.9, 2.0), (1.0, 1.04, 0.42e-3, 0.06, 0.9, 2.0), (1.5, 2.08, 0.83e-3, 0.2, 1.5, 3.3), (1.1, 2.0, 0.42e-3, 0.06, 0.9, 2.0),
+        (1.4, 1.2, 0.83e-3, 0.06, 0.9, 2.0), (1.0, 1.2, 0.42e-3, 0.12, 1.6, 4.0)]
+CYCLE = 0.83e-3
+
+
+def durations(ops, pace):
+    f, ga, pcy, wake, issue, flight = pace
+    out, first = [], 2.0
+    for o in ops:
+        k, n = o["ck"]
+        if k == "send":
+            out.append(issue + first)
+            first = 0.0
+        else:
+            out.append({"v": 0.03 + max(64, n) * CYCLE * f, "s": 0.05 + max(64, n) * CYCLE * f, "stab": 0.05 + (1.5 + n * CYCLE) * f, "gather": 0.06 + n * CYCLE * ga,
+                        "scatter": 0.05 + 3.8 * n * CYCLE, "mm": n * (pcy * f + 1e-4), "sel": (0.17 + 2 * n * CYCLE) * f, "ld": 1.6 + 1.6 * n, "net": flight, "us": n}[k])
+    return out
+
+
+def arrange(ops, rounds):
+    n = len(ops)
+    deps = [sorted(o["deps"]) for o in ops]
+    dset = [o["deps"] for o in ops]
+    qs = ["XVSPGY".index(o["q"]) for o in ops]
+    sets = []
+    for p in PACE:
+        c = durations(ops, p)
+        sets.append((c, [0.06 if o["kind"] == "dma" else x for o, x in zip(ops, c)], p[3]))
+    land = [o["name"] == "land" for o in ops]
+
+    def run(order, k, why=None):
+        c, hold, wake = sets[k]
+        fin, free, lastq = [0.0] * n, [0.0] * 6, [-1] * 6
+        for i in order:
+            s, a = 0.0, -1
+            for d in deps[i]:
+                if fin[d] > s:
+                    s, a = fin[d], d
+            q = qs[i]
+            if q:
+                if s > free[q]:
+                    s += wake
+                else:
+                    s = free[q]
+                    if lastq[q] != a:
+                        a = -2 - lastq[q]
+                free[q] = s + hold[i]
+                lastq[q] = i
+            elif land[i]:
+                s, a = 0.0, -1
+            fin[i] = s + c[i]
+            if why is not None:
+                why[i] = a
+        return fin
+
+    def pairs(order, k):
+        why = [0] * n
+        fin = run(order, k, why)
+        i, out = fin.index(max(fin)), []
+        while why[i] != -1:
+            if why[i] < -1:
+                if ops[i]["t"] not in PAR["lock"] and ops[-2 - why[i]]["t"] not in PAR["lock"]:
+                    out.append((-2 - why[i], i))
+                i = -2 - why[i]
+            else:
+                i = why[i]
+        return out
+
+    at = {(o["name"], o["t"], o["j"]): i for i, o in enumerate(ops)}
+
+    def named(text, t, only=""):
+        w = [(x.strip("+").split("."), t + x.count("+")) for x in text.split()]
+        return [at[k] for k in [(a, -1 if a == "exp" else s, int(j)) for (a, j), s in w] if k in at and (not only or ops[at[k]]["q"] == only)]
+
+    cycle = PAR["cycle"].split()
+    late = " ".join(cycle[cycle.index("G2.2"):])
+    middle = named(late, 0) + named(PAR["cycle"], 1) + named(PAR["cycle"], 2)
+    pred = [set(d) for d in deps]
+    for seq in [named(PAR["open"], 0, "S"), named(PAR["close"], ST - 1, "S")] + [[i for i in middle if qs[i] == q] for q in range(1, 6)]:
+        for a, b in zip(seq, seq[1:]):
+            pred[b].add(a)
+    succ = [[] for _ in ops]
+    for i, p in enumerate(pred):
+        for d in p:
+            succ[d].append(i)
+    c, hold, wake = sets[0]
+    left, prio, stack = [len(s) for s in succ], [0.0] * n, [i for i in range(n) if not succ[i]]
+    while stack:
+        i = stack.pop()
+        prio[i] = c[i] + max([prio[k] + wake for k in succ[i]] + [0.0])
+        for d in pred[i]:
+            left[d] -= 1
+            if not left[d]:
+                stack.append(d)
+    left, est, free, order = [len(p) for p in pred], [0.0] * n, [0.0] * 6, []
+    ready = [i for i in range(n) if not left[i]]
+    while ready:
+        start = [(max(est[i], free[qs[i]]), -prio[i], i) for i in ready]
+        s, _, i = min(start)
+        if qs[i]:
+            _, s, i = min((p, x, k) for x, p, k in start if qs[k] == qs[i] and x <= s + min(0.15, c[i]))
+            free[qs[i]] = s + hold[i]
+        ready.remove(i)
+        order.append(i)
+        for k in succ[i]:
+            left[k] -= 1
+            est[k] = max(est[k], (0.0 if land[i] else s) + c[i] + wake)
+            if not left[k]:
+                ready.append(k)
+
+    def move(order, u, v, back):
+        a, b = order.index(u), order.index(v)
+        seg = order[a:b + 1]
+        if back:
+            go, used = {v}, set()
+            need = set(dset[v])
+            for x in reversed(seg[:-1]):
+                if x in need or (x != u and qs[x] in used):
+                    go.add(x)
+                    need |= dset[x]
+                    if qs[x]:
+                        used.add(qs[x])
+            return None if u in go else order[:a] + [x for x in seg if x in go] + [x for x in seg if x not in go] + order[b + 1:]
+        go, used = {u}, set()
+        for x in seg[1:]:
+            if dset[x] & go or (x != v and qs[x] in used):
+                go.add(x)
+                if qs[x]:
+                    used.add(qs[x])
+        return None if v in go else order[:a] + [x for x in seg if x not in go] + [x for x in seg if x in go] + order[b + 1:]
+
+    seed = [PAR["seed"]]
+
+    def draw(k):
+        seed[0] = (seed[0] * 1103515245 + 12345) % 2147483648
+        return (seed[0] >> 8) % k
+
+    unit = [PAR["weights"][k] / max(run(order, k)) for k in range(len(sets))]
+    live = [k for k, u in enumerate(unit) if u]
+
+    def score(o, a, old):
+        total, new = 0.0, []
+        for m, k in enumerate(live):
+            c, hold, wake = sets[k]
+            fin, marks = old[m][0][:], old[m][1][:a // 32 + 1]
+            free = marks[-1][:]
+            for b in range(a // 32 * 32, n, 32):
+                for i in o[b:b + 32]:
+                    s = 0.0
+                    for d in deps[i]:
+                        if fin[d] > s:
+                            s = fin[d]
+                    q = qs[i]
+                    if q:
+                        s = s + wake if s > free[q] else free[q]
+                        free[q] = s + hold[i]
+                    elif land[i]:
+                        s = 0.0
+                    fin[i] = s + c[i]
+                marks.append(free[:])
+            total += unit[k] * max(fin)
+            new.append((fin, marks))
+        return total / sum(PAR["weights"]), new
+
+    now, state = score(order, 0, [([0.0] * n, [[0.0] * 6]) for k in live])
+    best, keep = now, order
+    crit = pairs(order, 0)
+    for r in range(rounds):
+        u, v = crit[draw(len(crit))]
+        back, k = draw(2), max(0, draw(5) - 1)
+        if k:
+            same = [x for x in order if qs[x] == qs[u]]
+            if back:
+                u = same[max(0, same.index(u) - k)]
+            else:
+                v = same[min(len(same) - 1, same.index(v) + k)]
+        o = move(order, u, v, back)
+        if o is None:
+            continue
+        s, new = score(o, order.index(u), state)
+        if s <= now - PAR["heat"] * (1 - r / rounds) * math.log((1 + draw(4096)) / 4096):
+            order, now, state = o, s, new
+            crit = pairs(order, live[draw(len(live))])
+            if s < best:
+                best, keep = s, o
+    return keep
 
 
 SEMOF = {"V": "vec", "S": "act", "P": "ten", "G": "gps"}
@@ -452,8 +684,9 @@ def rank_program(g, core, T, topo):
     if rank is None:
         return
     ops, nloc = build(g, T, topo, core, rank)
-    order, beg, fin = plan(ops)
-    emit(g, T, ops, order)
-    for k in range(NC + 1):
+    if "order" not in LAY:
+        LAY["order"] = arrange(ops, PAR["rounds"])
+    emit(g, T, ops, LAY["order"])
+    for k in range(len(LAY["chunks"]) + 1):
         g.wait_ge(T.sem["st%d" % k], 16)
     g.wait_ge(T.sem.loc, nloc[0])

@@ -6,13 +6,12 @@ W = 3584
 M = 224
 ST = 4
 NQ = 14
-CYC = ("G2.0 lnI.3 lnS.1 Rld.0 decI.3 G1.3 diff0.2 diff1.2 decS.1 scan3.0 Inew.0 R.0 min0.2 vote.0 s2.0 s1.0 neg0.3 gapc.0 min1.2 scan1.3 scan2.2 neg1.3 "
-       "G2.1 A.0 lnS.2 Tr.0 n0.2 decS.2 scan3.1 diff0.3 prep.1 Inew.1 R.1 diff1.3 col.2 min0.3 "
-       "G2.2 vote.1 s2.1 s1.1 n1.2 lnI.0+ gapc.2 prep.2 min1.3 Rld.2 scan2.3 lnS.3 decI.0+ G1.0+ base.1 Tr.2 scan3.2 prep.3 Inew.2 R.2 count.1 decS.3 c0.1 vote.2 "
-       "s1.2 s2.2 neg1.0+ spread.1 scan1.0+ c2.1 diff1.0+ "
-       "G2.3 A.1 c1.1 lnI.1+ Tsel.1 min1.0+ scan3.3 decI.1+ Inew.3 R.3 base.3 neg0.0+ diff0.0+ count.3 vote.3 scatter.1 min0.0+ c0.3 scan2.0+ s2.3 s1.3 spread.3 "
-       "A.2 B.1 G1.1+ lnI.2+ c2.3 c1.3 Tsel.3 lnS.0+ decI.2+ scan1.1+ decS.0+ scatter.3 G1.2+ neg1.1+ neg0.1+ diff1.1+ min1.1+ diff0.1+ min0.1+ n0.0+ scan2.1+ "
-       "prep.0+ neg0.2+ col.0+ n1.0+ scan1.2+ neg1.2+ A.3 B.3")
+CYC = ("scan1.2 G2.0 lnI.3 neg1.2 col.0 neg0.2 prep.0 diff0.2 n1.0 scan2.1 Rld.0 lnS.1 decI.3 G1.3 diff1.2 scan3.0 min0.2 n0.2 Inew.0 decS.1 min1.2 R.0 col.2 neg0.3 vote.0 "
+       "G2.1 n1.2 scan1.3 s1.0 s2.0 diff0.3 neg1.3 diff1.3 prep.1 gapc.0 scan2.2 A.0 min0.3 lnS.2 Rld.2 decS.2 scan3.1 "
+       "G2.2 min1.3 Inew.1 Tr.0 R.1 vote.1 gapc.2 scan2.3 lnS.3 s2.1 s1.1 prep.3 Tr.2 decS.3 scan3.2 prep.2 count.1 c0.1 Inew.2 R.2 base.1 vote.2 lnI.0+ decI.0+ spread.1 "
+       "G2.3 A.1 G1.0+ s2.2 s1.2 scan3.3 c2.1 Inew.3 scatter.1 R.3 scan1.0+ Tsel.1 c1.1 lnI.1+ neg0.0+ neg1.0+ vote.3 count.3 decI.1+ diff0.0+ s1.3 s2.3 c0.3 min0.0+ "
+       "diff1.0+ base.3 min1.0+ A.2 B.1 G1.1+ spread.3 c2.3 scan2.0+ lnI.2+ Tsel.3 c1.3 lnS.0+ decI.2+ scan1.1+ A.3 G1.2+ decS.0+ scatter.3 n0.0+ neg1.1+ neg0.1+ "
+       "diff1.1+ diff0.1+ B.3 min1.1+ min0.1+")
 PAR = {
     "sizes": [48, 64, 64, 48],
     "halves": [2, 2],
@@ -22,11 +21,11 @@ PAR = {
     "convc": "VGGGVV",
     "g1v": (2,), "g2v": (),
     "zq": "SS",
-    "tq": "S", "rq": "S", "uq": "S", "fold": True, "fin": 3,
+    "tq": "S", "rq": "S", "uq": "S", "from": (0, "G2.2"), "out": [112, 64], "gapat": 0, "yq": "Y",
     "open": "G1.0 exp.0 G1.1 exp.1 exp.2 exp.4 exp.3 exp.5 lnS.0 G2.0 G2.1 G1.3 G2.2 G2.3",
-    "close": "G2.0 G1.3 G2.1 G2.2 G2.3",
+    "close": "G1.3 G2.1 G2.2 G2.3",
     "cycle": CYC,
-    "lock": (2,), "weights": [3, 0, 1, 1, 0, 1], "rounds": 70000, "heat": 0.0007, "seed": 1,
+    "lock": (1, 2), "weights": [2, 0, 1, 1, 1], "rounds": 45000, "heat": 0.0007, "seed": 1,
 }
 KE = 512.0
 KV = float(2 ** 60)
@@ -68,35 +67,37 @@ def declare():
     sb("cf lf", W, "float32")
     sb("Cc", 2 * W, "bfloat16")
     sb("Lc", W, "bfloat16")
-    sb("cu32 il32 pt pa q16 cl c16", 2 * Q, "int32")
-    sb("gap32 Ri Ni", M, "int32")
-    sb("gapf gc0 gc1 gc2 lnI lnS lnR f2s", M, "float32")
-    sb("fo fi", M + 2 * Q, "float32")
+    sb("cu32 il32 q16 cl c16", 2 * Q, "int32")
+    sb("pt pa row", 128, "int32")
+    sb("gap32 Ni Ri", M, "int32")
+    sb("gapf gc0 gc1 gc2 lnI lnS", M, "float32")
+    sb("fo", M + Q, "float32")
     sb("cuin", NQ, "int32")
     sb("il", 2 * Q, "uint16")
+    sb("turn", 4 * Q, "uint16")
     sb("Iu su", M, "uint16")
     sb("Inew Rld R", M, "bfloat16")
     sb("mask", 16 * max(PAR["sizes"]), "bfloat16")
-    sb("idK idN bP bQ f1 id1 idW idA idB hb", 128, "bfloat16")
+    sb("idK idN bP bQ f1 id1 idA idB hb thr", 128, "bfloat16")
     sb("idF", 128, "float32")
-    sb("e3", 144, "bfloat16")
+    sb("blk", Q, "bfloat16")
+    sb("spl", 2 * Q, "bfloat16")
+    sb("f1s f2s fi", PAR["sizes"][-1] + Q, "float32")
     for h, (j0, j1, a, e) in enumerate(parts):
         n = e - a
-        sb("ni%d" % h, Q, "float32")
         sb("nw%d" % h, 2 * Q, "bfloat16")
         sb("cb%d" % h, 3 * Q, "bfloat16")
         sb("rl%d" % h, Q, "uint16")
         sb("ls%d" % h, 2 * Q, "uint16")
-        sb("mm%d" % h, Q, "bfloat16")
-        sb("idH%d" % h, 128, "bfloat16")
+        sb("mm%d" % h, 128, "bfloat16")
+        sb("sp%d" % h, 4 * Q, "bfloat16")
         for t in range(ST):
             sb("TW%d_%d" % (t, h), 2 * n + 4 * Q, "bfloat16")
             if t < ST - 1:
                 sb("MS%d_%d" % (t, h), n + 2 * Q, "bfloat16")
+    sb("Ic0", M, "bfloat16")
     for t in range(ST):
-        sb("Ic%d" % t, M, "bfloat16")
-        if t < ST - 1:
-            sb("IP%d s2%d" % (t, t), M, "bfloat16")
+        sb("Ic%d s1%d s2%d" % (t + 1, t, t), M + Q, "bfloat16")
     for j, n in enumerate(PAR["sizes"]):
         sb("x%d y%d P%d u%d z%d q%d" % (j, j, j, j, j, j), n * 16, "bfloat16")
     for k in range(8):
@@ -104,7 +105,7 @@ def declare():
     s = ["vec", "act", "ten", "gps", "loc", "gap"]
     for t in range(ST):
         s += ["a%d_%d" % (t, j) for j in range(len(chunks))] + ["b%d_%d" % (t, h) for h in range(len(parts))]
-    s += ["ld%d" % k for k in range(len(PAR["cp"]) + len(PAR["lp"]) + 2)] + ["st%d" % k for k in range(len(chunks) + 1)]
+    s += ["ld%d" % k for k in range(len(PAR["cp"]) + len(PAR["lp"]) + 2)] + ["st%d" % k for k in range(len(PAR["out"]))] + ["stc", "stl"]
     SEMAPHORES[:] = s
 
 
@@ -115,8 +116,7 @@ def build(g, T, topo, core, rank):
     A, F = AluOpType, ActivationFunctionType
     chunks, parts, LP, CP = LAY["chunks"], LAY["parts"], LAY["lp"], LAY["cp"]
     NC = len(chunks)
-    FIN = PAR["fin"]
-    YC = Q - NQ if FIN == 0 else Q + M
+    NL = chunks[-1][1] - chunks[-1][0]
     ops = []
     hist = {}
     at = [-1, 0]
@@ -153,7 +153,7 @@ def build(g, T, topo, core, rank):
 
     v, sc, te, sy = g.vector, g.scalar, g.tensor, g.sync
 
-    fills = [("id1", 1.0), ("bP", KV), ("e3", 1.0), ("f1", 1.0), ("mask", 1.0), ("cu32", 0)] + [("mm%d" % h, 0.0) for h in range(len(parts))]
+    fills = [("id1", 1.0), ("bP", KV), ("blk", 1.0), ("f1", 1.0), ("mask", 1.0), ("cu32", 0)]
     for b, c in fills:
         V(SCRATCH[b][1][1] / 2, lambda b=b, c=c: v.memset(T[b][:], c), [], [full(b)], "fill")
     V(64, lambda: v.memset(T.mask[:, 0::16], 0.0), [], [full("mask")], "fill")
@@ -163,21 +163,29 @@ def build(g, T, topo, core, rank):
     def sel(out, src, n, pattern, cmp, base, cm):
         op("G", ("sel", n), lambda: g.affine_select(T[out][:], T[src][:], pattern, cmp, 0.0, base, cm), [full(src)], [full(out)], name="sel")
 
-    op("G", ("us", 0.2), lambda: g.iota(T.pt[:], [[0, 2 * Q]], 0, 1), [], [full("pt")], name="iota")
+    op("G", ("us", 0.35), lambda: g.iota(T.pt[:], [[0, 128]], 0, 1), [], [full("pt")], name="iota")
+    op("G", ("us", 0.35), lambda: g.iota(T.row[:], [[0, 8], [1, 16]], 0, 0), [], [full("row")], name="iota")
     op("G", ("us", 0.2), lambda: g.iota(T.q16[:], [[16, 2 * Q]], 0, 0), [], [full("q16")], name="iota")
     sel("id1", "id1", 128, [[-1, 128]], A.is_equal, 0, 1)
     sel("bP", "bP", 128, [[-16, 8], [0, 16]], A.is_ge, 0, 1)
     sel("bP", "bP", 128, [[16, 8], [0, 16]], A.is_ge, 15, -1)
-    sel("e3", "e3", 144, [[0, 9], [1, 16]], A.is_equal, -15, 0)
-    sel("e3", "e3", 144, [[-16, 9], [0, 16]], A.is_ge, 0, 1)
-    sel("e3", "e3", 144, [[16, 9], [0, 16]], A.is_ge, 15, -1)
-    scaled = [("idN", "id1", -KE), ("idK", "id1", KE), ("idF", "id1", 1.0), ("idW", "id1", -float(W)), ("idA", "id1", 16.0), ("idB", "id1", -16.0), ("bQ", "bP", -1.0)]
-    for o, f, c in scaled + [("idH%d" % h, "id1", -float(e - a)) for h, (j0, j1, a, e) in enumerate(parts)]:
+    sel("blk", "blk", Q, [[-16, Q]], A.is_ge, 0, 1)
+    sel("blk", "blk", Q, [[16, Q]], A.is_ge, 15, -1)
+    for o, f, c in [("idN", "id1", -KE), ("idK", "id1", KE), ("idF", "id1", 1.0), ("idA", "id1", 16.0), ("idB", "id1", -16.0), ("bQ", "bP", -1.0)]:
         V(128, lambda o=o, f=f, c=c: v.tensor_scalar(T[o][:], T[f][:], c, None, A.mult), [full(f)], [full(o)], "k")
+    for h, (j0, j1, a, e) in enumerate(parts):
+        for k, c in enumerate((1.0, 1.0, -float(e - a), -float(W))):
+            V(Q, lambda h=h, k=k, c=c: v.tensor_scalar(T["sp%d" % h][:, k * Q:k * Q + Q], T.blk[:], c, None, A.mult), [full("blk")], [("sp%d" % h, k * Q, k * Q + Q)], "k")
 
-    V(NQ, lambda: v.tensor_scalar(T.pa[:], T.pt[:], 15, None, A.bitwise_and), [full("pt")], [full("pa")], "k")
-    V(NQ, lambda: v.tensor_tensor(T.cl[:], T.pa[:], T.q16[:], A.add), [full("pa"), full("q16")], [full("cl")], "k")
+    for k, c in enumerate((-KE, KE)):
+        V(Q, lambda k=k, c=c: v.tensor_scalar(T.spl[:, k * Q:k * Q + Q], T.blk[:], c, None, A.mult), [full("blk")], [("spl", k * Q, k * Q + Q)], "k")
+    V(128, lambda: v.tensor_scalar(T.pa[:], T.pt[:], 15, None, A.bitwise_and), [full("pt")], [full("pa")], "k")
+    V(256, lambda: v.tensor_tensor(T.pt[:], T.pa[:], T.row[:], A.not_equal), [full("pa"), full("row")], [full("pt")], "k")
+    V(128, lambda: v.tensor_scalar(T.thr[:], T.pt[:], 60.0 * KV, 3.5 * KV, A.mult, A.add), [full("pt")], [full("thr")], "k")
+    V(NQ, lambda: v.tensor_tensor(T.cl[:], T.pa[:, 0:2 * Q], T.q16[:], A.add), [full("pa"), full("q16")], [full("cl")], "k")
     V(NQ, lambda: v.tensor_scalar(T.c16[:], T.cl[:], 16.0, None, A.mult), [full("cl")], [full("c16")], "k")
+    for k in range(2):
+        V(NQ, lambda k=k: v.tensor_scalar(T.turn[:, 2 * Q * k:2 * Q * k + 2 * Q], T.cl[:], 32.0 * Q * k, None, A.add), [full("cl")], [("turn", 2 * Q * k, 2 * Q * k + 2 * Q)], "k")
     for h, (j0, j1, a, e) in enumerate(parts):
         n, q0, cb = e - a, a // 16, T["cb%d" % h]
         CB = "cb%d" % h
@@ -202,9 +210,10 @@ def build(g, T, topo, core, rank):
 
     load(T.cuin[:], T.cu[:], "cuin", 0, NQ)
     V(NQ, lambda: v.tensor_copy(T.cu32[:, 0:NQ], T.cuin[:]), [full("cuin")], [full("cu32")], "k")
-    load(T.gap32[:], T.gap[:], "gap32", 0, M)
     lead = PAR["lead"]
-    for src, (lo, hi) in [("ck", x) for x in CP[:lead]] + [("la", x) for x in LP] + [("ck", x) for x in CP[lead:]]:
+    pieces = [("ck", x) for x in CP[:lead]] + [("la", x) for x in LP] + [("ck", x) for x in CP[lead:]]
+    pieces.insert(PAR["gapat"], ("gap", (0, M)))
+    for src, (lo, hi) in pieces:
         load(T[src + "32"][:, lo:hi], T[src][:, lo:hi], src + "32", lo, hi)
 
     for h, (j0, j1, a, e) in enumerate(parts):
@@ -225,18 +234,22 @@ def build(g, T, topo, core, rank):
         gather("V", T.Iu[:, a:e], T.ck32[:, 0:16 * e], first(a, e), e - a, [("ck32", 0, 16 * e), full("il")], [("Iu", a, e)], "Iu0")
     exps = []
 
-    def encode(src, f, o, lo, hi, q):
+    def encode(src, f, o, lo, hi, q, k="s"):
+        if q == "S":
+            exps.append(op("S", ("gather", hi - lo), lambda: sc.activation(T[o][:, lo:hi], T[src][:, lo:hi].indirect(T.turn[:, 0:(hi - lo) // 16]), F.Exp, bias=B0, scale=1.0 / SC),
+                           [(src, lo, hi), full("turn")], [(o, lo, hi)], name="exp"))
+            return
         if q == "V":
             V(hi - lo, lambda: v.tensor_copy(T[f][:, lo:hi], T[src][:, lo:hi]), [(src, lo, hi)], [(f, lo, hi)], "conv")
         else:
             op("G", ("sel", hi - lo), lambda: g.affine_select(T[f][:, lo:hi], T[src][:, lo:hi], [[0, hi - lo]], A.is_ge, 0.0, 0, 0), [(src, lo, hi)], [(f, lo, hi)], name="conv")
-        exps.append(S(hi - lo, lambda: sc.activation(T[o][:, lo:hi], T[f][:, lo:hi], F.Exp, bias=B0, scale=1.0 / SC), [(f, lo, hi)], [(o, lo, hi)], name="exp"))
+        exps.append(S(hi - lo, lambda: sc.activation(T[o][:, lo:hi], T[f][:, lo:hi], F.Exp, bias=B0, scale=1.0 / SC), [(f, lo, hi)], [(o, lo, hi)], name="exp", k=k))
 
     V(M, lambda: v.tensor_scalar(T.gapf[:], T.gap32[:], 0.5, None, A.subtract), [full("gap32")], [full("gapf")], "gapf")
-    exps.append(S(M, lambda: sc.activation(T.gc0[:], T.gapf[:], F.Exp, scale=1.0 / SC), [full("gapf")], [full("gc0")], name="expg", k="stab"))
+    exps.append(S(M, lambda: sc.activation(T.gc0[:], T.gapf[:], F.Exp, scale=1.0 / SC), [full("gapf")], [full("gc0")], name="expg", k="s" if PAR["gapat"] else "stab"))
     for k, (lo, hi) in enumerate(LP):
         at[1] = 10 + k
-        encode("la32", "lf", "Lc", lo, hi, "V")
+        encode("la32", "lf", "Lc", lo, hi, "V", "stab" if PAR["gapat"] and not k else "s")
     for j, (a, e) in enumerate(cuts(PAR["cp"])):
         at[1] = j
         encode("ck32", "cf", "Cc", 16 * a, 16 * e, PAR["convc"][j])
@@ -267,7 +280,7 @@ def build(g, T, topo, core, rank):
                 g.remote_dma_fused([RemoteDMATransfer(dst_ids=[DstId(rid=a[0], pnc=a[1])], dma_engine_mask=topo.mask(core, nxt), remote_sem=T.sem[sem],
                                                       srcs=[T[b][:, c:c + hi - lo] for b, c in srcs], dsts=[T[dst][:, lo:hi]], alu_op=2)], local_sem=T.sem.loc)
         i = op("G", ("send", 1), fn, [(b, c, c + hi - lo) for b, c in srcs], [], kind="send", name=name)
-        op("X", ("net", 1), None, [], [(dst, lo, hi)], sem=(sem, ne), kind="arr", deps=[i], name="arr" + name)
+        op("X", ("net", len(srcs)), None, [], [(dst, lo, hi)], sem=(sem, ne), kind="arr", deps=[i], name="arr" + name)
 
     gn, cn = "ps6", "ps7"
     pg, pc = T[gn], T[cn]
@@ -284,10 +297,10 @@ def build(g, T, topo, core, rank):
             V(n, lambda: v.tensor_scalar(T.Iu[:, a:e], T.lnI[:, a:e], SC, OFF + 0.25, A.mult, A.add), [("lnI", a, e)], [("Iu", a, e)], "decI")
         gather("V" if t == 0 and j in PAR["g1v"] else "S", xb[:], T.Lc[:], T.Iu[:, a:e], 16 * n, [full("Lc"), ("Iu", a, e)], [full(X)], "G1")
         V(8 * n, lambda: v.tensor_tensor_scan(Pb[:], T.mask[:, 0:16 * n], xb[:], 0.0, A.mult, A.max), [full("mask"), full(X)], [full(P)], "scan1")
-        k = -(-n * 16 // 512)
+        k = 2
         per = 16 // k
         for h in range(k):
-            b = "ps%d" % (2 * (j % 2) + h)
+            b = "ps%d" % (2 * ((t * NC + j) % 2) + h)
 
             op("P", ("mm", per * n), lambda h=h, pb=T[b]: te.matmul(pb[:, 0:per * n], T.idN[:], xb[:, h::k], True, False), [full("idN"), full(X)], [full(b)], name="neg%d" % h)
 
@@ -329,9 +342,6 @@ def build(g, T, topo, core, rank):
         gather(PAR["zq"][1] if t == 0 else PAR["rq"], T.Rld[:, a:e], T.Cc[:, 0:W], T[RL][:, 0:nq], n, [("Cc", 0, W), full(RL)], [("Rld", a, e)], "Rld")
         if not last:
             V(n, lambda: v.tensor_tensor(tw[:, 0:n], T.Rld[:, a:e], pg[:, a:e], A.mult), [("Rld", a, e), full(gn)], [(TW, 0, n)], "Tr")
-        else:
-            S(n, lambda: sc.activation(T.lnR[:, a:e], T.Rld[:, a:e], F.Ln, scale=UP), [("Rld", a, e)], [("lnR", a, e)], name="lnR")
-            V(n, lambda: v.tensor_scalar(T.Ri[:, a:e], T.lnR[:, a:e], SC, OFF, A.mult, A.add), [("lnR", a, e)], [("Ri", a, e)], "decR")
 
     def join(t, j):
         a, e = chunks[j]
@@ -340,7 +350,7 @@ def build(g, T, topo, core, rank):
         last = t == ST - 1
         h = [k for k, p in enumerate(parts) if p[0] <= j < p[1]][0]
         TW, c = "TW%d_%d" % (t, h), parts[h][3] - 2 * parts[h][2]
-        IC, Z, QB, pn = "Ic%d" % t, "z%d" % j, "q%d" % j, "ps%d" % (4 + j % 2)
+        IC, Z, QB, pn = "Ic%d" % t, "z%d" % j, "q%d" % j, "ps%d" % (4 + (t * NC + j) % 2)
         zb, qb, pb = T[Z], T[QB], T[pn]
 
         def prep():
@@ -359,43 +369,40 @@ def build(g, T, topo, core, rank):
             return te.matmul(pb[:, 64:64 + n], T.bQ[:], T.R[:, a:e], False, True)
 
         op("P", ("mm", 128), votes, [full("bP"), full("bQ"), ("R", a, e)], [full(pn)], name="vote")
-        if last:
-            S(n, lambda: sc.activation(T.lnI[:, a:e], T.Inew[:, a:e], F.Ln, scale=UP), [("Inew", a, e)], [("lnI", a, e)], name="lnN")
-            V(n, lambda: v.tensor_scalar(T.Ni[:, a:e], T.lnI[:, a:e], SC, OFF, A.mult, A.add), [("lnI", a, e)], [("Ni", a, e)], "decN")
-            new, rld, s2, out, dst = "Ni", "Ri", "f2s", "fo", "fi"
-        else:
-            new, rld, s2, out, dst = "Inew", "Rld", "s2%d" % t, "IP%d" % t, "Ic%d" % (t + 1)
-        V(n, lambda: v.tensor_tensor(T[s2][:, a:e], T[new][:, a:e], pb[:, 64:64 + n], A.min), [(new, a, e), full(pn)], [(s2, a, e)], "s2")
-        if PAR["fold"] and not last:
-            V(n, lambda: v.tensor_tensor(T[out][:, a:e], T[rld][:, a:e], pb[:, 0:n], A.min), [(rld, a, e), full(pn)], [(out, a, e)], "s1")
-            send("A", "a%d_%d" % (t, j), dst, a, e, [(out, a), (s2, a)])
+        s1, s2 = "s1%d" % t, "s2%d" % t
+        if last and j == NC - 1:
+            for src, ln, whole, out, w, x in (("Rld", "lnS", "Ri", "f1s", 0, "R"), ("Inew", "lnI", "Ni", "f2s", 64, "N")):
+                S(n, lambda src=src, ln=ln: sc.activation(T[ln][:, a:e], T[src][:, a:e], F.Ln, scale=UP), [(src, a, e)], [(ln, a, e)], name="ln" + x)
+                V(n, lambda ln=ln, whole=whole: v.tensor_scalar(T[whole][:, a:e], T[ln][:, a:e], SC, OFF, A.mult, A.add), [(ln, a, e)], [(whole, a, e)], "dec" + x)
+                V(n, lambda whole=whole, out=out, w=w: v.tensor_tensor(T[out][:, 0:n], T[whole][:, a:e], pb[:, w:w + n], A.min), [(whole, a, e), full(pn)], [(out, 0, n)], "s2" if w else "s1")
             return
-        V(n, lambda: v.tensor_tensor(pb[:, 128:128 + n], T[rld][:, a:e], pb[:, 0:n], A.min), [(rld, a, e), full(pn)], [full(pn)], "s1")
-        o = Q if last else 0
-        V(n, lambda: v.tensor_tensor(T[out][:, o + a:o + e], T[s2][:, a:e], pb[:, 128:128 + n], A.max), [full(pn), (s2, a, e)], [(out, o + a, o + e)], "IP")
-        if not (last and j == FIN):
-            send("A", "a%d_%d" % (t, j), dst, o + a, o + e, [(out, o + a)])
+        V(n, lambda: v.tensor_tensor(T[s2][:, a:e], T.Inew[:, a:e], pb[:, 64:64 + n], A.min), [("Inew", a, e), full(pn)], [(s2, a, e)], "s2")
+        V(n, lambda: v.tensor_tensor(T[s1][:, a:e], T.Rld[:, a:e], pb[:, 0:n], A.min), [("Rld", a, e), full(pn)], [(s1, a, e)], "s1")
+        send("A", "a%d_%d" % (t, j), "Ic%d" % (t + 1), a, e, [(s1, a), (s2, a)])
 
     def lists(t, h):
         j0, j1, a, e = parts[h]
         at[:] = [t, j1 - 1]
         last = t == ST - 1
         n, nq = e - a, (e - a) // 16
-        TW, MS, LS, MM, NI, NW = "TW%d_%d" % (t, h), "MS%d_%d" % (t, h), "ls%d" % h, "mm%d" % h, "ni%d" % h, "nw%d" % h
+        TW, MS, LS, MM, NW = "TW%d_%d" % (t, h), "MS%d_%d" % (t, h), "ls%d" % h, "mm%d" % h, "nw%d" % h
         tw, c = T[TW], 2 * n
 
-        def count():
-            for p in range(16):
-                r = te.matmul(pg[:, 256:256 + nq], T.e3[:, 15 - p:143 - p], T.R[:, a + p:e:16], p == 0, p == 15)
-            return r
-
-        op("P", ("mm", 1024), count, [full("e3"), ("R", a, e)], [full(gn)], name="count")
-        V(Q, lambda: v.tensor_scalar(T[MM][:, 0:nq], pg[:, 256:256 + nq], 3.5, None, A.is_ge), [full(gn)], [full(MM)], "c0")
+        SP = "sp%d" % h
+        op("P", ("mm", 128), lambda: te.matmul(pg[0:n, 256:384], T.R[:, a:e], T.bP[:], True, True), [full("bP"), ("R", a, e)], [full(gn)], name="count")
+        V(128, lambda: v.tensor_tensor(T[MM][0:n, :], T.thr[0:n, :], pg[0:n, 256:384], A.is_le), [full(gn), full("thr")], [full(MM)], "c0")
         if last:
-            op("P", ("mm", 64), lambda: te.matmul(pc[:, 0:Q], T.id1[:], tw[:, c:c + Q], True, False), [full("id1"), (TW, c, c + Q)], [full(cn)], name="base")
-            op("P", ("mm", 64), lambda: te.matmul(pc[:, 0:Q], T.id1[:], T[MM][:], False, True), [full("id1"), full(MM)], [full(cn)], name="spread")
-            V(Q, lambda: v.tensor_scalar(T[NI][:], pc[:, 0:Q], 15.5, -16.0, A.is_ge, A.mult), [full(cn)], [full(NI)], "c1")
-            V(Q, lambda: v.tensor_tensor(T.fo[:, YC + a // 16:YC + e // 16], T[NI][:, 0:nq], pc[:, 0:nq], A.add), [full(NI), full(cn)], [("fo", YC + a // 16, YC + e // 16)], "c2")
+            lo, hi = NL + a // 16, NL + e // 16
+
+            def both():
+                te.matmul(pc[:, 0:2 * Q], T.id1[:], tw[:, c:c + 2 * Q], True, False)
+                te.matmul(pc[:, 0:2 * Q], T.idB[:], T[NW][:], False, False)
+                return te.matmul(pc[:, Q:2 * Q], T.idN[:], T.f1[:, 0:Q], False, False)
+
+            op("P", ("mm", 192), both, [full("id1"), full("idB"), full("idN"), full("f1"), full(NW), (TW, c, c + 2 * Q)], [full(cn)], name="base")
+            op("P", ("mm", 64), lambda: te.matmul(pc[:, 0:2 * Q], T[MM][0:n, :], T.spl[0:n, :], False, True), [full("spl"), full(MM)], [full(cn)], name="spread")
+            V(Q, lambda: v.tensor_copy(T.f2s[:, lo:hi], pc[:, 0:nq]), [full(cn)], [("f2s", lo, hi)], "c1")
+            V(Q, lambda: v.tensor_copy(T.f1s[:, lo:hi], pc[:, Q:Q + nq]), [full(cn)], [("f1s", lo, hi)], "c2")
             return
 
         def base():
@@ -404,13 +411,8 @@ def build(g, T, topo, core, rank):
             te.matmul(pc[:, 3 * Q:4 * Q], T.idA[:], T["cb%d" % h][:, 0:Q], False, False)
             return te.matmul(pc[:, 3 * Q:4 * Q], T.idB[:], T[NW][:, 0:Q], False, False)
 
-        def spread():
-            for k, w in enumerate(("id1", "id1", "idH%d" % h, "idW")):
-                r = te.matmul(pc[:, k * Q:k * Q + Q], T[w][:], T[MM][:], False, k == 3)
-            return r
-
         op("P", ("mm", 256), base, [full("id1"), full("idA"), full("idB"), full("cb%d" % h), full(NW), (TW, c, c + 4 * Q)], [full(cn)], name="base")
-        op("P", ("mm", 256), spread, [full("id1"), full("idW"), full("idH%d" % h), full(MM)], [full(cn)], name="spread")
+        op("P", ("mm", 64), lambda: te.matmul(pc[:, 0:4 * Q], T[MM][0:n, :], T[SP][0:n, :], False, True), [full(SP), full(MM)], [full(cn)], name="spread")
         ms = T[MS]
         V(2 * Q, lambda: v.tensor_copy(T[LS][:], pc[:, 2 * Q:4 * Q]), [full(cn)], [full(LS)], "c2")
         if PAR["uq"] == "S":
@@ -431,33 +433,33 @@ def build(g, T, topo, core, rank):
             first_acquires(t, j)
         for h in range(len(parts)):
             reloads(t, h)
-        todo = list(range(NC)) if t < ST - 1 else [j for j in range(NC) if j != FIN] + [FIN]
-        for k, j in enumerate(todo):
-            join(t, j)
-            for h, (j0, j1, a, e) in enumerate(parts):
-                if j0 <= j < j1 and not [x for x in todo[k + 1:] if j0 <= x < j1]:
-                    lists(t, h)
+        for h, (j0, j1, a, e) in enumerate(parts):
+            for j in range(j0, j1):
+                join(t, j)
+            lists(t, h)
         if t < ST - 1:
             for h in range(len(parts)):
                 scatter(t, h)
-    a, e = chunks[FIN]
-    at[:] = [ST - 1, FIN]
-    lo, hi = (Q - NQ, Q + e) if FIN == 0 else (Q + a, Q + M + NQ)
-    send("A", "a%d_%d" % (ST - 1, FIN), "fi", lo, hi, [("fo", lo)])
-    at[:] = [ST, 0]
-    for j, (a, e) in enumerate(chunks):
-        op("Y", ("us", 1.9), lambda a=a, e=e: sy.dma_start(T.yi[:, a:e], T.fi[:, Q + a:Q + e]), [("fi", Q + a, Q + e)], [], sem="st%d" % j, kind="dma", name="yi")
-    op("S", ("us", 1.9), lambda: sc.dma_start(T.yc[:], T.fi[:, YC:YC + NQ]), [("fi", YC, YC + NQ)], [], sem="st%d" % NC, kind="dma", name="yc")
+    a, IC = chunks[-1][0], "Ic%d" % ST
+    send("A", "a%d_%d" % (ST - 1, NC - 1), "fi", 0, NL + NQ, [("f1s", 0), ("f2s", 0)])
+    for j, (a, e) in enumerate(cuts(PAR["out"])):
+        at[:] = [ST, j]
+        S(e - a, lambda a=a, e=e: sc.activation(T.lnI[:, a:e], T[IC][:, a:e], F.Ln, scale=UP), [(IC, a, e)], [("lnI", a, e)], name="lnY")
+        V(e - a, lambda a=a, e=e: v.tensor_scalar(T.Ni[:, a:e], T.lnI[:, a:e], SC, OFF, A.mult, A.add), [("lnI", a, e)], [("Ni", a, e)], "decY")
+        V(e - a, lambda a=a, e=e: v.tensor_copy(T.fo[:, a:e], T.Ni[:, a:e]), [("Ni", a, e)], [("fo", a, e)], "outY")
+        op("Y", ("us", 1.9), lambda a=a, e=e: sy.dma_start(T.yi[:, a:e], T.fo[:, a:e]), [("fo", a, e)], [], sem="st%d" % j, kind="dma", name="yi")
+    op("Y", ("us", 1.9), lambda: sy.dma_start(T.yi[:, M - NL:M], T.fi[:, 0:NL]), [("fi", 0, NL)], [], sem="stl", kind="dma", name="yl")
+    op(PAR["yq"], ("us", 1.9), lambda: (sc if PAR["yq"] == "S" else sy).dma_start(T.yc[:], T.fi[:, NL:NL + NQ]), [("fi", NL, NL + NQ)], [], sem="stc", kind="dma", name="yc")
     return ops, nloc
 
 
-PACE = [(1.05, 1.56, 0.42e-3, 0.08, 0.9, 2.0), (1.0, 1.04, 0.42e-3, 0.06, 0.9, 2.0), (1.5, 2.08, 0.83e-3, 0.2, 1.5, 3.3), (1.1, 2.0, 0.42e-3, 0.06, 0.9, 2.0),
-        (1.4, 1.2, 0.83e-3, 0.06, 0.9, 2.0), (1.0, 1.2, 0.42e-3, 0.12, 1.6, 4.0)]
+PACE = [(1.0, 1.5, 0.35e-3, -0.18, 0.5, 1.9, 0.0), (1.15, 1.56, 0.35e-3, -0.15, 0.5, 1.9, 0.0), (1.35, 1.9, 0.55e-3, -0.25, 0.9, 2.7, 0.0),
+        (1.0, 2.05, 0.35e-3, -0.12, 0.5, 1.9, 0.0), (1.1, 1.4, 0.35e-3, -0.2, 1.0, 2.9, 0.0)]
 CYCLE = 0.83e-3
 
 
 def durations(ops, pace):
-    f, ga, pcy, wake, issue, flight = pace
+    f, ga, pcy, wake, issue, flight, fix = pace
     out, first = [], 2.0
     for o in ops:
         k, n = o["ck"]
@@ -465,8 +467,8 @@ def durations(ops, pace):
             out.append(issue + first)
             first = 0.0
         else:
-            out.append({"v": 0.03 + max(64, n) * CYCLE * f, "s": 0.05 + max(64, n) * CYCLE * f, "stab": 0.05 + (1.5 + n * CYCLE) * f, "gather": 0.06 + n * CYCLE * ga,
-                        "scatter": 0.05 + 3.8 * n * CYCLE, "mm": n * (pcy * f + 1e-4), "sel": (0.17 + 2 * n * CYCLE) * f, "ld": 1.6 + 1.6 * n, "net": flight, "us": n}[k])
+            out.append({"v": fix + max(64, n) * CYCLE * f, "s": 0.02 + fix + max(64, n) * CYCLE * f, "stab": 0.05 + (1.5 + n * CYCLE) * f, "gather": 0.06 + n * CYCLE * ga,
+                        "scatter": 0.05 + 3.8 * n * CYCLE, "mm": n * (pcy * f + 1e-4), "sel": (0.17 + 2 * n * CYCLE) * f, "ld": 1.6 + 1.6 * n, "net": flight + 0.45 * (n - 2), "us": n}[k])
     return out
 
 
@@ -491,8 +493,8 @@ def arrange(ops, rounds):
                     s, a = fin[d], d
             q = qs[i]
             if q:
-                if s > free[q]:
-                    s += wake
+                if s - min(wake, 0.0) > free[q]:
+                    s += abs(wake)
                 else:
                     s = free[q]
                     if lastq[q] != a:
@@ -522,12 +524,14 @@ def arrange(ops, rounds):
     at = {(o["name"], o["t"], o["j"]): i for i, o in enumerate(ops)}
 
     def named(text, t, only=""):
-        w = [(x.strip("+").split("."), t + x.count("+")) for x in text.split()]
+        w = [(x.strip("+-").split("."), t + x.count("+") - x.count("-")) for x in text.split()]
         return [at[k] for k in [(a, -1 if a == "exp" else s, int(j)) for (a, j), s in w] if k in at and (not only or ops[at[k]]["q"] == only)]
 
     cycle = PAR["cycle"].split()
-    late = " ".join(cycle[cycle.index("G2.2"):])
-    middle = named(late, 0) + named(PAR["cycle"], 1) + named(PAR["cycle"], 2)
+    t0, w0 = PAR["from"]
+    middle = named(" ".join(cycle[cycle.index(w0):]), t0)
+    for t in range(t0 + 1, ST - 1):
+        middle += named(PAR["cycle"], t)
     pred = [set(d) for d in deps]
     for seq in [named(PAR["open"], 0, "S"), named(PAR["close"], ST - 1, "S")] + [[i for i in middle if qs[i] == q] for q in range(1, 6)]:
         for a, b in zip(seq, seq[1:]):
@@ -595,6 +599,7 @@ def arrange(ops, rounds):
         total, new = 0.0, []
         for m, k in enumerate(live):
             c, hold, wake = sets[k]
+            late, soon = abs(wake), -min(wake, 0.0)
             fin, marks = old[m][0][:], old[m][1][:a // 32 + 1]
             free = marks[-1][:]
             for b in range(a // 32 * 32, n, 32):
@@ -605,7 +610,7 @@ def arrange(ops, rounds):
                             s = fin[d]
                     q = qs[i]
                     if q:
-                        s = s + wake if s > free[q] else free[q]
+                        s = s + late if s + soon > free[q] else free[q]
                         free[q] = s + hold[i]
                     elif land[i]:
                         s = 0.0
@@ -687,6 +692,8 @@ def rank_program(g, core, T, topo):
     if "order" not in LAY:
         LAY["order"] = arrange(ops, PAR["rounds"])
     emit(g, T, ops, LAY["order"])
-    for k in range(len(LAY["chunks"]) + 1):
+    for k in range(len(PAR["out"])):
         g.wait_ge(T.sem["st%d" % k], 16)
+    g.wait_ge(T.sem.stc, 16)
+    g.wait_ge(T.sem.stl, 16)
     g.wait_ge(T.sem.loc, nloc[0])

import math
from concourse.bass import DstId, RemoteDMATransfer
from concourse.mybir import AluOpType, ActivationFunctionType

W = 3584
M = 224
ST = 4
NQ = 14
CYC = ("scan1.2 G2.0 lnI.3 neg1.2 col.0 neg0.2 prep.0 diff0.2 n1.0 scan2.1 Rld.0 lnS.1 decI.3 G1.3 diff1.2 scan3.0 min0.2 n0.2 Inew.0 decS.1 min1.2 R.0 col.2 neg0.3 vote.0 "
       "G2.1 n1.2 scan1.3 s1.0 s2.0 diff0.3 neg1.3 diff1.3 prep.1 gapc.0 scan2.2 A.0 min0.3 lnS.2 Rld.2 decS.2 scan3.1 "
       "G2.2 min1.3 Inew.1 Tr.0 R.1 vote.1 gapc.2 scan2.3 lnS.3 s2.1 s1.1 prep.3 Tr.2 decS.3 scan3.2 prep.2 count.1 c0.1 Inew.2 R.2 base.1 vote.2 lnI.0+ decI.0+ spread.1 "
       "G2.3 A.1 G1.0+ s2.2 s1.2 scan3.3 c2.1 Inew.3 scatter.1 R.3 scan1.0+ Tsel.1 c1.1 lnI.1+ neg0.0+ neg1.0+ vote.3 count.3 decI.1+ diff0.0+ s1.3 s2.3 c0.3 min0.0+ "
       "diff1.0+ base.3 min1.0+ A.2 B.1 G1.1+ spread.3 c2.3 scan2.0+ lnI.2+ Tsel.3 c1.3 lnS.0+ decI.2+ scan1.1+ A.3 G1.2+ decS.0+ scatter.3 n0.0+ neg1.1+ neg0.1+ "
       "diff1.1+ diff0.1+ B.3 min1.1+ min0.1+")
PAR = {
    "sizes": [48, 64, 64, 48],
    "halves": [2, 2],
    "lp": [1024, 1024, 1024, 512],
    "cp": [48, 64, 32, 32, 32, 16],
    "lead": 0,
    "convc": "VGGGVV",
    "g1v": (2,), "g2v": (),
    "zq": "SS",
    "tq": "S", "rq": "S", "uq": "S", "from": (0, "G2.2"), "out": [112, 64], "gapat": 0, "yq": "Y",
    "open": "G1.0 exp.0 G1.1 exp.1 exp.2 exp.4 exp.3 exp.5 lnS.0 G2.0 G2.1 G1.3 G2.2 G2.3",
    "close": "G1.3 G2.1 G2.2 G2.3",
    "cycle": CYC,
    "lock": (1, 2), "weights": [2, 0, 1, 1, 1], "rounds": 45000, "heat": 0.0007, "seed": 1,
}
KE = 512.0
KV = float(2 ** 60)
SC = 32.0 / math.log(2.0)
SHIFT = 45.0 / 64
B0 = (SHIFT / 32 - 100.0) * math.log(2.0)
UP = 2.0 ** 50
OFF = 1600.0 - SHIFT
EPS = 2.0 ** -62
Q = 16

SCRATCH = {}
SEMAPHORES = []
LAY = {}


def cuts(sizes):
    out, a = [], 0
    for n in sizes:
        out.append((a, a + n))
        a += n
    return out


def declare():
    SCRATCH.clear()
    chunks = cuts(PAR["sizes"])
    parts, j = [], 0
    for k in PAR["halves"]:
        parts.append((j, j + k, chunks[j][0], chunks[j + k - 1][1]))
        j += k
    LAY.update(chunks=chunks, parts=parts, lp=cuts(PAR["lp"]), cp=[(16 * a, 16 * e) for a, e in cuts(PAR["cp"])])

    def sb(names, n, t):
        for x in names.split():
            SCRATCH[x] = ("sbuf", [128, n], t)

    sb("ck32 la32", W, "int32")
    sb("cf lf", W, "float32")
    sb("Cc", 2 * W, "bfloat16")
    sb("Lc", W, "bfloat16")
    sb("cu32 il32 q16 cl c16", 2 * Q, "int32")
    sb("pt pa row", 128, "int32")
    sb("gap32 Ni Ri", M, "int32")
    sb("gapf gc0 gc1 gc2 lnI lnS", M, "float32")
    sb("fo", M + Q, "float32")
    sb("cuin", NQ, "int32")
    sb("il", 2 * Q, "uint16")
    sb("turn", 4 * Q, "uint16")
    sb("Iu su", M, "uint16")
    sb("Inew Rld R", M, "bfloat16")
    sb("mask", 16 * max(PAR["sizes"]), "bfloat16")
    sb("idK idN bP bQ f1 id1 idA idB hb thr", 128, "bfloat16")
    sb("idF", 128, "float32")
    sb("blk", Q, "bfloat16")
    sb("spl", 2 * Q, "bfloat16")
    sb("f1s f2s fi", PAR["sizes"][-1] + Q, "float32")
    for h, (j0, j1, a, e) in enumerate(parts):
        n = e - a
        sb("nw%d" % h, 2 * Q, "bfloat16")
        sb("cb%d" % h, 3 * Q, "bfloat16")
        sb("rl%d" % h, Q, "uint16")
        sb("ls%d" % h, 2 * Q, "uint16")
        sb("mm%d" % h, 128, "bfloat16")
        sb("sp%d" % h, 4 * Q, "bfloat16")
        for t in range(ST):
            sb("TW%d_%d" % (t, h), 2 * n + 4 * Q, "bfloat16")
            if t < ST - 1:
                sb("MS%d_%d" % (t, h), n + 2 * Q, "bfloat16")
    sb("Ic0", M, "bfloat16")
    for t in range(ST):
        sb("Ic%d s1%d s2%d" % (t + 1, t, t), M + Q, "bfloat16")
    for j, n in enumerate(PAR["sizes"]):
        sb("x%d y%d P%d u%d z%d q%d" % (j, j, j, j, j, j), n * 16, "bfloat16")
    for k in range(8):
        SCRATCH["ps%d" % k] = ("psum", [128, 512], "float32")
    s = ["vec", "act", "ten", "gps", "loc", "gap"]
    for t in range(ST):
        s += ["a%d_%d" % (t, j) for j in range(len(chunks))] + ["b%d_%d" % (t, h) for h in range(len(parts))]
    s += ["ld%d" % k for k in range(len(PAR["cp"]) + len(PAR["lp"]) + 2)] + ["st%d" % k for k in range(len(PAR["out"]))] + ["stc", "stl"]
    SEMAPHORES[:] = s


declare()


def build(g, T, topo, core, rank):
    A, F = AluOpType, ActivationFunctionType
    chunks, parts, LP, CP = LAY["chunks"], LAY["parts"], LAY["lp"], LAY["cp"]
    NC = len(chunks)
    NL = chunks[-1][1] - chunks[-1][0]
    ops = []
    hist = {}
    at = [-1, 0]

    def op(q, ck, fn, reads=(), writes=(), sem=None, deps=(), kind="c", name=""):
        i = len(ops)
        dd = set(deps)
        for lst, wr in ((reads, False), (writes, True)):
            for (b, lo, hi) in lst:
                for (l2, h2, k, w2) in hist.get(b, ()):
                    if k != i and l2 < hi and lo < h2 and (wr or w2):
                        dd.add(k)
        for (b, lo, hi) in writes:
            h = hist.get(b, [])
            hist[b] = [e for e in h if not (lo <= e[0] and e[1] <= hi)] + [(lo, hi, i, True)]
        for (b, lo, hi) in reads:
            hist.setdefault(b, []).append((lo, hi, i, False))
        ops.append({"q": q, "ck": ck, "fn": fn, "deps": dd, "sem": sem, "kind": kind, "name": name, "t": at[0], "j": at[1]})
        return i

    def V(n, fn, reads, writes, name=""):
        return op("V", ("v", n), fn, reads, writes, name=name)

    def S(n, fn, reads, writes, name="", deps=(), k="s"):
        return op("S", (k, n), fn, reads, writes, name=name, deps=deps)

    def gather(q, out, win, lst, n, reads, writes, name):
        if q == "S":
            return op("S", ("gather", n), lambda: sc.activation(out, win.indirect(lst), F.Copy), reads, writes, name=name)
        return op("V", ("gather", n), lambda: v.tensor_copy(out, win.indirect(lst)), reads, writes, name=name)

    def full(b):
        return (b, 0, 1 << 20)

    v, sc, te, sy = g.vector, g.scalar, g.tensor, g.sync

    fills = [("id1", 1.0), ("bP", KV), ("blk", 1.0), ("f1", 1.0), ("mask", 1.0), ("cu32", 0)]
    for b, c in fills:
        V(SCRATCH[b][1][1] / 2, lambda b=b, c=c: v.memset(T[b][:], c), [], [full(b)], "fill")
    V(64, lambda: v.memset(T.mask[:, 0::16], 0.0), [], [full("mask")], "fill")
    V(64, lambda: v.memset(T.hb[:, 0:64], -3.5 * KV), [], [("hb", 0, 64)], "fill")
    V(64, lambda: v.memset(T.hb[:, 64:128], 3.5 * KV), [], [("hb", 64, 128)], "fill")

    def sel(out, src, n, pattern, cmp, base, cm):
        op("G", ("sel", n), lambda: g.affine_select(T[out][:], T[src][:], pattern, cmp, 0.0, base, cm), [full(src)], [full(out)], name="sel")

    op("G", ("us", 0.35), lambda: g.iota(T.pt[:], [[0, 128]], 0, 1), [], [full("pt")], name="iota")
    op("G", ("us", 0.35), lambda: g.iota(T.row[:], [[0, 8], [1, 16]], 0, 0), [], [full("row")], name="iota")
    op("G", ("us", 0.2), lambda: g.iota(T.q16[:], [[16, 2 * Q]], 0, 0), [], [full("q16")], name="iota")
    sel("id1", "id1", 128, [[-1, 128]], A.is_equal, 0, 1)
    sel("bP", "bP", 128, [[-16, 8], [0, 16]], A.is_ge, 0, 1)
    sel("bP", "bP", 128, [[16, 8], [0, 16]], A.is_ge, 15, -1)
    sel("blk", "blk", Q, [[-16, Q]], A.is_ge, 0, 1)
    sel("blk", "blk", Q, [[16, Q]], A.is_ge, 15, -1)
    for o, f, c in [("idN", "id1", -KE), ("idK", "id1", KE), ("idF", "id1", 1.0), ("idA", "id1", 16.0), ("idB", "id1", -16.0), ("bQ", "bP", -1.0)]:
        V(128, lambda o=o, f=f, c=c: v.tensor_scalar(T[o][:], T[f][:], c, None, A.mult), [full(f)], [full(o)], "k")
    for h, (j0, j1, a, e) in enumerate(parts):
        for k, c in enumerate((1.0, 1.0, -float(e - a), -float(W))):
            V(Q, lambda h=h, k=k, c=c: v.tensor_scalar(T["sp%d" % h][:, k * Q:k * Q + Q], T.blk[:], c, None, A.mult), [full("blk")], [("sp%d" % h, k * Q, k * Q + Q)], "k")

    for k, c in enumerate((-KE, KE)):
        V(Q, lambda k=k, c=c: v.tensor_scalar(T.spl[:, k * Q:k * Q + Q], T.blk[:], c, None, A.mult), [full("blk")], [("spl", k * Q, k * Q + Q)], "k")
    V(128, lambda: v.tensor_scalar(T.pa[:], T.pt[:], 15, None, A.bitwise_and), [full("pt")], [full("pa")], "k")
    V(256, lambda: v.tensor_tensor(T.pt[:], T.pa[:], T.row[:], A.not_equal), [full("pa"), full("row")], [full("pt")], "k")
    V(128, lambda: v.tensor_scalar(T.thr[:], T.pt[:], 60.0 * KV, 3.5 * KV, A.mult, A.add), [full("pt")], [full("thr")], "k")
    V(NQ, lambda: v.tensor_tensor(T.cl[:], T.pa[:, 0:2 * Q], T.q16[:], A.add), [full("pa"), full("q16")], [full("cl")], "k")
    V(NQ, lambda: v.tensor_scalar(T.c16[:], T.cl[:], 16.0, None, A.mult), [full("cl")], [full("c16")], "k")
    for k in range(2):
        V(NQ, lambda k=k: v.tensor_scalar(T.turn[:, 2 * Q * k:2 * Q * k + 2 * Q], T.cl[:], 32.0 * Q * k, None, A.add), [full("cl")], [("turn", 2 * Q * k, 2 * Q * k + 2 * Q)], "k")
    for h, (j0, j1, a, e) in enumerate(parts):
        n, q0, cb = e - a, a // 16, T["cb%d" % h]
        CB = "cb%d" % h
        V(NQ, lambda cb=cb, q0=q0: v.tensor_copy(cb[:, 0:Q], T.cl[:, q0:q0 + Q]), [full("cl")], [(CB, 0, Q)], "k")
        V(NQ, lambda cb=cb, n=n: v.tensor_scalar(cb[:, Q:2 * Q], T.cl[:, 0:Q], float(n), None, A.add), [full("cl")], [(CB, Q, 2 * Q)], "k")
        V(NQ, lambda cb=cb: v.memset(cb[:, 2 * Q:3 * Q], float(W)), [], [(CB, 2 * Q, 3 * Q)], "k")
        for t in range(ST - 1):
            b = "TW%d_%d" % (t, h)
            V(NQ, lambda b=b, n=n, cb=cb: v.tensor_copy(T[b][:, 2 * n + 2 * Q:2 * n + 4 * Q], cb[:, Q:3 * Q]), [full(CB)], [(b, 2 * n + 2 * Q, 2 * n + 4 * Q)], "k")

    nld = [0]
    amount = [0]
    prev = []

    def load(out, in_, b, lo, hi):
        k = nld[0]
        nld[0] += 1
        amount[0] += hi - lo
        i = op("Y", ("us", 0.06), lambda: sy.dma_start(out, in_), [], [(b, lo, hi)], sem="ld%d" % k, kind="dma", name="ld", deps=prev[-1:])
        prev.append(i)
        op("X", ("ld", amount[0] / 896.0), None, [], [(b, lo, hi)], sem=("ld%d" % k, 16), kind="arr", deps=[i], name="land")

    load(T.cuin[:], T.cu[:], "cuin", 0, NQ)
    V(NQ, lambda: v.tensor_copy(T.cu32[:, 0:NQ], T.cuin[:]), [full("cuin")], [full("cu32")], "k")
    lead = PAR["lead"]
    pieces = [("ck", x) for x in CP[:lead]] + [("la", x) for x in LP] + [("ck", x) for x in CP[lead:]]
    pieces.insert(PAR["gapat"], ("gap", (0, M)))
    for src, (lo, hi) in pieces:
        load(T[src + "32"][:, lo:hi], T[src][:, lo:hi], src + "32", lo, hi)

    for h, (j0, j1, a, e) in enumerate(parts):
        n, q0, b = e - a, a // 16, "TW0_%d" % h
        for k in range(2):
            V(NQ, lambda b=b, n=n, q0=q0, k=k: v.tensor_scalar(T[b][:, 2 * n + k * Q:2 * n + k * Q + Q], T.cu32[:, q0:q0 + Q], float(k), None, A.add),
              [full("cu32")], [(b, 2 * n + k * Q, 2 * n + k * Q + Q)], "k")
    V(NQ, lambda: v.tensor_tensor(T.il32[:, 0:Q], T.cu32[:, 0:Q], T.c16[:, 0:Q], A.add), [full("cu32"), full("c16")], [full("il32")], "il")
    V(NQ, lambda: v.tensor_copy(T.il[:, 0:NQ], T.il32[:, 0:NQ]), [full("il32")], [("il", 0, Q)], "il")
    V(NQ, lambda: v.tensor_copy(T.il[:, Q + 1:Q + 1 + NQ], T.il32[:, 0:NQ]), [full("il32")], [("il", Q, 2 * Q)], "il")

    def first(a, e):
        o = (Q + 1) * (a // 16 % 2)
        return T.il[:, o + a // 16:o + e // 16]

    for j, (a, e) in enumerate(chunks):
        at[1] = j
        gather("V", T.Iu[:, a:e], T.ck32[:, 0:16 * e], first(a, e), e - a, [("ck32", 0, 16 * e), full("il")], [("Iu", a, e)], "Iu0")
    exps = []

    def encode(src, f, o, lo, hi, q, k="s"):
        if q == "S":
            exps.append(op("S", ("gather", hi - lo), lambda: sc.activation(T[o][:, lo:hi], T[src][:, lo:hi].indirect(T.turn[:, 0:(hi - lo) // 16]), F.Exp, bias=B0, scale=1.0 / SC),
                           [(src, lo, hi), full("turn")], [(o, lo, hi)], name="exp"))
            return
        if q == "V":
            V(hi - lo, lambda: v.tensor_copy(T[f][:, lo:hi], T[src][:, lo:hi]), [(src, lo, hi)], [(f, lo, hi)], "conv")
        else:
            op("G", ("sel", hi - lo), lambda: g.affine_select(T[f][:, lo:hi], T[src][:, lo:hi], [[0, hi - lo]], A.is_ge, 0.0, 0, 0), [(src, lo, hi)], [(f, lo, hi)], name="conv")
        exps.append(S(hi - lo, lambda: sc.activation(T[o][:, lo:hi], T[f][:, lo:hi], F.Exp, bias=B0, scale=1.0 / SC), [(f, lo, hi)], [(o, lo, hi)], name="exp", k=k))

    V(M, lambda: v.tensor_scalar(T.gapf[:], T.gap32[:], 0.5, None, A.subtract), [full("gap32")], [full("gapf")], "gapf")
    exps.append(S(M, lambda: sc.activation(T.gc0[:], T.gapf[:], F.Exp, scale=1.0 / SC), [full("gapf")], [full("gc0")], name="expg", k="s" if PAR["gapat"] else "stab"))
    for k, (lo, hi) in enumerate(LP):
        at[1] = 10 + k
        encode("la32", "lf", "Lc", lo, hi, "V", "stab" if PAR["gapat"] and not k else "s")
    for j, (a, e) in enumerate(cuts(PAR["cp"])):
        at[1] = j
        encode("ck32", "cf", "Cc", 16 * a, 16 * e, PAR["convc"][j])

    nloc = [0]
    cores = list(T.cores)
    nxt = cores[(rank + 1) % len(cores)]
    ne = len(topo.engines(core, nxt))

    def send_gap():
        dst = [cores[(rank + d) % len(cores)] for d in (1, 2)]
        eng = [e for e in topo.engines(core, dst[0]) if e in topo.engines(core, dst[1])]
        ids = [DstId(rid=topo.addr(d)[0], pnc=topo.addr(d)[1]) for d in dst]
        nloc[0] += len(eng)
        g.remote_dma_fused([RemoteDMATransfer(dst_ids=ids, dma_engine_mask=sum(1 << e for e in eng), remote_sem=T.sem.gap, srcs=[T.gc0[:]], dsts=[T.gc1[:], T.gc2[:]])], local_sem=T.sem.loc)

    i = op("G", ("send", 1), send_gap, [full("gc0")], [], kind="send", name="gap")
    op("X", ("us", 5.0), None, [], [full("gc1"), full("gc2")], sem=("gap", 2 * ne), kind="arr", deps=[i], name="agap")

    def send(name, sem, dst, lo, hi, srcs):
        def fn():
            a = topo.addr(nxt)
            nloc[0] += ne
            if len(srcs) == 1:
                b, c = srcs[0]
                g.remote_dma(T[dst][:, lo:hi], T[b][:, c:c + hi - lo], T.sem[sem], T.sem.loc, a[1], a[0], topo.mask(core, nxt))
            else:
                g.remote_dma_fused([RemoteDMATransfer(dst_ids=[DstId(rid=a[0], pnc=a[1])], dma_engine_mask=topo.mask(core, nxt), remote_sem=T.sem[sem],
                                                      srcs=[T[b][:, c:c + hi - lo] for b, c in srcs], dsts=[T[dst][:, lo:hi]], alu_op=2)], local_sem=T.sem.loc)
        i = op("G", ("send", 1), fn, [(b, c, c + hi - lo) for b, c in srcs], [], kind="send", name=name)
        op("X", ("net", len(srcs)), None, [], [(dst, lo, hi)], sem=(sem, ne), kind="arr", deps=[i], name="arr" + name)

    gn, cn = "ps6", "ps7"
    pg, pc = T[gn], T[cn]

    def first_acquires(t, j):
        a, e = chunks[j]
        n = e - a
        at[:] = [t, j]
        IC = "Ic%d" % t
        xb, yb, Pb, ub = T["x%d" % j], T["y%d" % j], T["P%d" % j], T["u%d" % j]
        X, Y, P, U = "x%d" % j, "y%d" % j, "P%d" % j, "u%d" % j
        if t > 0:
            S(n, lambda: sc.activation(T.lnI[:, a:e], T[IC][:, a:e], F.Ln, scale=UP), [(IC, a, e)], [("lnI", a, e)], name="lnI")
            V(n, lambda: v.tensor_scalar(T.Iu[:, a:e], T.lnI[:, a:e], SC, OFF + 0.25, A.mult, A.add), [("lnI", a, e)], [("Iu", a, e)], "decI")
        gather("V" if t == 0 and j in PAR["g1v"] else "S", xb[:], T.Lc[:], T.Iu[:, a:e], 16 * n, [full("Lc"), ("Iu", a, e)], [full(X)], "G1")
        V(8 * n, lambda: v.tensor_tensor_scan(Pb[:], T.mask[:, 0:16 * n], xb[:], 0.0, A.mult, A.max), [full("mask"), full(X)], [full(P)], "scan1")
        k = 2
        per = 16 // k
        for h in range(k):
            b = "ps%d" % (2 * ((t * NC + j) % 2) + h)

            op("P", ("mm", per * n), lambda h=h, pb=T[b]: te.matmul(pb[:, 0:per * n], T.idN[:], xb[:, h::k], True, False), [full("idN"), full(X)], [full(b)], name="neg%d" % h)

            def diff(h=h, pb=T[b]):
                for i in range(per):
                    r = te.matmul(pb[:, i:per * n:per], T.idK[:], Pb[:, 15::16], False, i == per - 1)
                return r

            op("P", ("mm", per * max(n, 64)), diff, [full("idK"), full(P)], [full(b)], name="diff%d" % h)
            V(per * n, lambda h=h, pb=T[b]: v.tensor_tensor(yb[:, h::k], xb[:, h::k], pb[:, 0:per * n], A.min), [full(X), full(b)], [(Y, h, h + 1)], "min%d" % h)
        V(8 * n, lambda: v.tensor_tensor_scan(ub[:], T.mask[:, 0:16 * n], yb[:], 0.0, A.mult, A.max), [full("mask"), full(Y)], [full(U)], "scan2")
        S(n, lambda: sc.activation(T.lnS[:, a:e], ub[:, 15::16], F.Ln, bias=EPS, scale=UP), [full(U)], [("lnS", a, e)],
          deps=exps if t == 0 else (), name="lnS", k="stab" if t == 0 and j == 0 else "s")
        V(n, lambda: v.tensor_scalar(T.su[:, a:e], T.lnS[:, a:e], SC, OFF + 0.25, A.mult, A.add), [("lnS", a, e)], [("su", a, e)], "decS")

    def reloads(t, h):
        j0, j1, a, e = parts[h]
        at[:] = [t, j0]
        last = t == ST - 1
        n, nq = e - a, (e - a) // 16
        TW, NW, RL = "TW%d_%d" % (t, h), "nw%d" % h, "rl%d" % h
        tw, c = T[TW], 2 * n
        if t == 0:
            gather(PAR["zq"][0], T.Ic0[:, a:e], T.Cc[:, 0:16 * e], first(a, e), n, [("Cc", 0, 16 * e), full("il")], [("Ic0", a, e)], "Ic0")
        if not last:
            gb = "gc%d" % t
            op("P", ("mm", 4 * n), lambda: te.matmul(pg[:, a:e], T.idF[:], T[gb][:, a:e], True, True), [full("idF"), full(gb)], [full(gn)], name="gapc")
            if t == 0:
                V(n, lambda: v.tensor_tensor(tw[:, n:c], T.Ic0[:, a:e], pg[:, a:e], A.mult), [("Ic0", a, e), full(gn)], [(TW, n, c)], "Tc0")
        V(2 * Q, lambda: v.tensor_scalar(T[NW][:], tw[:, c:c + 2 * Q], 15.5, None, A.is_ge), [(TW, c, c + 2 * Q)], [full(NW)], "n0")

        def column():
            te.matmul(pc[:, 128:128 + Q], T.id1[:], tw[:, c + Q:c + 2 * Q], True, False)
            te.matmul(pc[:, 128:128 + Q], T.idA[:], T["cb%d" % h][:, 0:Q], False, False)
            return te.matmul(pc[:, 128:128 + Q], T.idB[:], T[NW][:, Q:2 * Q], False, True)

        op("P", ("mm", 192), column, [full("id1"), full("idA"), full("idB"), full("cb%d" % h), full(NW), (TW, c, c + 2 * Q)], [full(cn)], name="col")
        V(Q, lambda: v.tensor_copy(T[RL][:], pc[:, 128:128 + Q]), [full(cn)], [full(RL)], "n1")
        gather(PAR["zq"][1] if t == 0 else PAR["rq"], T.Rld[:, a:e], T.Cc[:, 0:W], T[RL][:, 0:nq], n, [("Cc", 0, W), full(RL)], [("Rld", a, e)], "Rld")
        if not last:
            V(n, lambda: v.tensor_tensor(tw[:, 0:n], T.Rld[:, a:e], pg[:, a:e], A.mult), [("Rld", a, e), full(gn)], [(TW, 0, n)], "Tr")

    def join(t, j):
        a, e = chunks[j]
        n = e - a
        at[:] = [t, j]
        last = t == ST - 1
        h = [k for k, p in enumerate(parts) if p[0] <= j < p[1]][0]
        TW, c = "TW%d_%d" % (t, h), parts[h][3] - 2 * parts[h][2]
        IC, Z, QB, pn = "Ic%d" % t, "z%d" % j, "q%d" % j, "ps%d" % (4 + (t * NC + j) % 2)
        zb, qb, pb = T[Z], T[QB], T[pn]

        def prep():
            te.matmul(pb[:, 256:256 + n], T.id1[:], T[IC][:, a:e], True, True)
            te.matmul(pb[:, 320:320 + n], T.id1[:], T[TW][:, c + a:c + e], True, True)
            return te.matmul(pb[:, 0:128], T.f1[0:1, :], T.hb[0:1, :], True, False)

        op("P", ("mm", 256), prep, [full("id1"), full("f1"), full("hb"), (IC, a, e), (TW, c + a, c + e)], [full(pn)], name="prep")
        gather("V" if t == 0 and j in PAR["g2v"] else "S", zb[:], T.Cc[:, 0:W], T.su[:, a:e], 16 * n, [("Cc", 0, W), ("su", a, e)], [full(Z)], "G2")
        V(8 * n, lambda: v.tensor_tensor_scan(qb[:], T.mask[:, 0:16 * n], zb[:], 0.0, A.mult, A.max), [full("mask"), full(Z)], [full(QB)], "scan3")
        V(n, lambda: v.tensor_tensor(T.Inew[:, a:e], qb[:, 15::16], pb[:, 256:256 + n], A.max), [full(pn), full(QB)], [("Inew", a, e)], "Inew")
        V(n, lambda: v.tensor_tensor(T.R[:, a:e], T.Inew[:, a:e], pb[:, 320:320 + n], A.is_ge), [("Inew", a, e), full(pn)], [("R", a, e)], "R")

        def votes():
            te.matmul(pb[:, 0:n], T.bP[:], T.R[:, a:e], False, False)
            return te.matmul(pb[:, 64:64 + n], T.bQ[:], T.R[:, a:e], False, True)

        op("P", ("mm", 128), votes, [full("bP"), full("bQ"), ("R", a, e)], [full(pn)], name="vote")
        s1, s2 = "s1%d" % t, "s2%d" % t
        if last and j == NC - 1:
            for src, ln, whole, out, w, x in (("Rld", "lnS", "Ri", "f1s", 0, "R"), ("Inew", "lnI", "Ni", "f2s", 64, "N")):
                S(n, lambda src=src, ln=ln: sc.activation(T[ln][:, a:e], T[src][:, a:e], F.Ln, scale=UP), [(src, a, e)], [(ln, a, e)], name="ln" + x)
                V(n, lambda ln=ln, whole=whole: v.tensor_scalar(T[whole][:, a:e], T[ln][:, a:e], SC, OFF, A.mult, A.add), [(ln, a, e)], [(whole, a, e)], "dec" + x)
                V(n, lambda whole=whole, out=out, w=w: v.tensor_tensor(T[out][:, 0:n], T[whole][:, a:e], pb[:, w:w + n], A.min), [(whole, a, e), full(pn)], [(out, 0, n)], "s2" if w else "s1")
            return
        V(n, lambda: v.tensor_tensor(T[s2][:, a:e], T.Inew[:, a:e], pb[:, 64:64 + n], A.min), [("Inew", a, e), full(pn)], [(s2, a, e)], "s2")
        V(n, lambda: v.tensor_tensor(T[s1][:, a:e], T.Rld[:, a:e], pb[:, 0:n], A.min), [("Rld", a, e), full(pn)], [(s1, a, e)], "s1")
        send("A", "a%d_%d" % (t, j), "Ic%d" % (t + 1), a, e, [(s1, a), (s2, a)])

    def lists(t, h):
        j0, j1, a, e = parts[h]
        at[:] = [t, j1 - 1]
        last = t == ST - 1
        n, nq = e - a, (e - a) // 16
        TW, MS, LS, MM, NW = "TW%d_%d" % (t, h), "MS%d_%d" % (t, h), "ls%d" % h, "mm%d" % h, "nw%d" % h
        tw, c = T[TW], 2 * n

        SP = "sp%d" % h
        op("P", ("mm", 128), lambda: te.matmul(pg[0:n, 256:384], T.R[:, a:e], T.bP[:], True, True), [full("bP"), ("R", a, e)], [full(gn)], name="count")
        V(128, lambda: v.tensor_tensor(T[MM][0:n, :], T.thr[0:n, :], pg[0:n, 256:384], A.is_le), [full(gn), full("thr")], [full(MM)], "c0")
        if last:
            lo, hi = NL + a // 16, NL + e // 16

            def both():
                te.matmul(pc[:, 0:2 * Q], T.id1[:], tw[:, c:c + 2 * Q], True, False)
                te.matmul(pc[:, 0:2 * Q], T.idB[:], T[NW][:], False, False)
                return te.matmul(pc[:, Q:2 * Q], T.idN[:], T.f1[:, 0:Q], False, False)

            op("P", ("mm", 192), both, [full("id1"), full("idB"), full("idN"), full("f1"), full(NW), (TW, c, c + 2 * Q)], [full(cn)], name="base")
            op("P", ("mm", 64), lambda: te.matmul(pc[:, 0:2 * Q], T[MM][0:n, :], T.spl[0:n, :], False, True), [full("spl"), full(MM)], [full(cn)], name="spread")
            V(Q, lambda: v.tensor_copy(T.f2s[:, lo:hi], pc[:, 0:nq]), [full(cn)], [("f2s", lo, hi)], "c1")
            V(Q, lambda: v.tensor_copy(T.f1s[:, lo:hi], pc[:, Q:Q + nq]), [full(cn)], [("f1s", lo, hi)], "c2")
            return

        def base():
            te.matmul(pc[:, 0:4 * Q], T.id1[:], tw[:, c:c + 4 * Q], True, False)
            te.matmul(pc[:, 3 * Q:4 * Q], T.id1[:], tw[:, c:c + Q], False, False)
            te.matmul(pc[:, 3 * Q:4 * Q], T.idA[:], T["cb%d" % h][:, 0:Q], False, False)
            return te.matmul(pc[:, 3 * Q:4 * Q], T.idB[:], T[NW][:, 0:Q], False, False)

        op("P", ("mm", 256), base, [full("id1"), full("idA"), full("idB"), full("cb%d" % h), full(NW), (TW, c, c + 4 * Q)], [full(cn)], name="base")
        op("P", ("mm", 64), lambda: te.matmul(pc[:, 0:4 * Q], T[MM][0:n, :], T[SP][0:n, :], False, True), [full(SP), full(MM)], [full(cn)], name="spread")
        ms = T[MS]
        V(2 * Q, lambda: v.tensor_copy(T[LS][:], pc[:, 2 * Q:4 * Q]), [full(cn)], [full(LS)], "c2")
        if PAR["uq"] == "S":
            S(2 * Q, lambda: sc.activation(ms[:, n:n + 2 * Q], pc[:, 0:2 * Q], F.Copy), [], [full(cn), (MS, n, n + 2 * Q)], name="c1")
        else:
            V(2 * Q, lambda: v.tensor_copy(ms[:, n:n + 2 * Q], pc[:, 0:2 * Q]), [full(cn)], [(MS, n, n + 2 * Q)], "c1")
        gather(PAR["tq"], ms[:, 0:n], tw[:, 0:c], T[LS][:, 0:nq], n, [(TW, 0, c), full(LS)], [(MS, 0, n)], "Tsel")
        send("B", "b%d_%d" % (t, h), "TW%d_%d" % (t + 1, h), n, c + 2 * Q, [(MS, 0)])

    def scatter(t, h):
        j0, j1, a, e = parts[h]
        at[:] = [t, j1 - 1]
        LS = "ls%d" % h
        op("V", ("scatter", e - a), lambda: v.tensor_copy(T.Cc[:].indirect(T[LS][:, Q:Q + (e - a) // 16]), T.Inew[:, a:e]), [("Inew", a, e), full(LS)], [full("Cc")], name="scatter")

    for t in range(ST):
        for j in range(NC):
            first_acquires(t, j)
        for h in range(len(parts)):
            reloads(t, h)
        for h, (j0, j1, a, e) in enumerate(parts):
            for j in range(j0, j1):
                join(t, j)
            lists(t, h)
        if t < ST - 1:
            for h in range(len(parts)):
                scatter(t, h)
    a, IC = chunks[-1][0], "Ic%d" % ST
    send("A", "a%d_%d" % (ST - 1, NC - 1), "fi", 0, NL + NQ, [("f1s", 0), ("f2s", 0)])
    for j, (a, e) in enumerate(cuts(PAR["out"])):
        at[:] = [ST, j]
        S(e - a, lambda a=a, e=e: sc.activation(T.lnI[:, a:e], T[IC][:, a:e], F.Ln, scale=UP), [(IC, a, e)], [("lnI", a, e)], name="lnY")
        V(e - a, lambda a=a, e=e: v.tensor_scalar(T.Ni[:, a:e], T.lnI[:, a:e], SC, OFF, A.mult, A.add), [("lnI", a, e)], [("Ni", a, e)], "decY")
        V(e - a, lambda a=a, e=e: v.tensor_copy(T.fo[:, a:e], T.Ni[:, a:e]), [("Ni", a, e)], [("fo", a, e)], "outY")
        op("Y", ("us", 1.9), lambda a=a, e=e: sy.dma_start(T.yi[:, a:e], T.fo[:, a:e]), [("fo", a, e)], [], sem="st%d" % j, kind="dma", name="yi")
    op("Y", ("us", 1.9), lambda: sy.dma_start(T.yi[:, M - NL:M], T.fi[:, 0:NL]), [("fi", 0, NL)], [], sem="stl", kind="dma", name="yl")
    op(PAR["yq"], ("us", 1.9), lambda: (sc if PAR["yq"] == "S" else sy).dma_start(T.yc[:], T.fi[:, NL:NL + NQ]), [("fi", NL, NL + NQ)], [], sem="stc", kind="dma", name="yc")
    return ops, nloc


PACE = [(1.0, 1.5, 0.35e-3, -0.18, 0.5, 1.9, 0.0), (1.15, 1.56, 0.35e-3, -0.15, 0.5, 1.9, 0.0), (1.35, 1.9, 0.55e-3, -0.25, 0.9, 2.7, 0.0),
        (1.0, 2.05, 0.35e-3, -0.12, 0.5, 1.9, 0.0), (1.1, 1.4, 0.35e-3, -0.2, 1.0, 2.9, 0.0)]
CYCLE = 0.83e-3


def durations(ops, pace):
    f, ga, pcy, wake, issue, flight, fix = pace
    out, first = [], 2.0
    for o in ops:
        k, n = o["ck"]
        if k == "send":
            out.append(issue + first)
            first = 0.0
        else:
            out.append({"v": fix + max(64, n) * CYCLE * f, "s": 0.02 + fix + max(64, n) * CYCLE * f, "stab": 0.05 + (1.5 + n * CYCLE) * f, "gather": 0.06 + n * CYCLE * ga,
                        "scatter": 0.05 + 3.8 * n * CYCLE, "mm": n * (pcy * f + 1e-4), "sel": (0.17 + 2 * n * CYCLE) * f, "ld": 1.6 + 1.6 * n, "net": flight + 0.45 * (n - 2), "us": n}[k])
    return out


def arrange(ops, rounds):
    n = len(ops)
    deps = [sorted(o["deps"]) for o in ops]
    dset = [o["deps"] for o in ops]
    qs = ["XVSPGY".index(o["q"]) for o in ops]
    sets = []
    for p in PACE:
        c = durations(ops, p)
        sets.append((c, [0.06 if o["kind"] == "dma" else x for o, x in zip(ops, c)], p[3]))
    land = [o["name"] == "land" for o in ops]

    def run(order, k, why=None):
        c, hold, wake = sets[k]
        fin, free, lastq = [0.0] * n, [0.0] * 6, [-1] * 6
        for i in order:
            s, a = 0.0, -1
            for d in deps[i]:
                if fin[d] > s:
                    s, a = fin[d], d
            q = qs[i]
            if q:
                if s - min(wake, 0.0) > free[q]:
                    s += abs(wake)
                else:
                    s = free[q]
                    if lastq[q] != a:
                        a = -2 - lastq[q]
                free[q] = s + hold[i]
                lastq[q] = i
            elif land[i]:
                s, a = 0.0, -1
            fin[i] = s + c[i]
            if why is not None:
                why[i] = a
        return fin

    def pairs(order, k):
        why = [0] * n
        fin = run(order, k, why)
        i, out = fin.index(max(fin)), []
        while why[i] != -1:
            if why[i] < -1:
                if ops[i]["t"] not in PAR["lock"] and ops[-2 - why[i]]["t"] not in PAR["lock"]:
                    out.append((-2 - why[i], i))
                i = -2 - why[i]
            else:
                i = why[i]
        return out

    at = {(o["name"], o["t"], o["j"]): i for i, o in enumerate(ops)}

    def named(text, t, only=""):
        w = [(x.strip("+-").split("."), t + x.count("+") - x.count("-")) for x in text.split()]
        return [at[k] for k in [(a, -1 if a == "exp" else s, int(j)) for (a, j), s in w] if k in at and (not only or ops[at[k]]["q"] == only)]

    cycle = PAR["cycle"].split()
    t0, w0 = PAR["from"]
    middle = named(" ".join(cycle[cycle.index(w0):]), t0)
    for t in range(t0 + 1, ST - 1):
        middle += named(PAR["cycle"], t)
    pred = [set(d) for d in deps]
    for seq in [named(PAR["open"], 0, "S"), named(PAR["close"], ST - 1, "S")] + [[i for i in middle if qs[i] == q] for q in range(1, 6)]:
        for a, b in zip(seq, seq[1:]):
            pred[b].add(a)
    succ = [[] for _ in ops]
    for i, p in enumerate(pred):
        for d in p:
            succ[d].append(i)
    c, hold, wake = sets[0]
    left, prio, stack = [len(s) for s in succ], [0.0] * n, [i for i in range(n) if not succ[i]]
    while stack:
        i = stack.pop()
        prio[i] = c[i] + max([prio[k] + wake for k in succ[i]] + [0.0])
        for d in pred[i]:
            left[d] -= 1
            if not left[d]:
                stack.append(d)
    left, est, free, order = [len(p) for p in pred], [0.0] * n, [0.0] * 6, []
    ready = [i for i in range(n) if not left[i]]
    while ready:
        start = [(max(est[i], free[qs[i]]), -prio[i], i) for i in ready]
        s, _, i = min(start)
        if qs[i]:
            _, s, i = min((p, x, k) for x, p, k in start if qs[k] == qs[i] and x <= s + min(0.15, c[i]))
            free[qs[i]] = s + hold[i]
        ready.remove(i)
        order.append(i)
        for k in succ[i]:
            left[k] -= 1
            est[k] = max(est[k], (0.0 if land[i] else s) + c[i] + wake)
            if not left[k]:
                ready.append(k)

    def move(order, u, v, back):
        a, b = order.index(u), order.index(v)
        seg = order[a:b + 1]
        if back:
            go, used = {v}, set()
            need = set(dset[v])
            for x in reversed(seg[:-1]):
                if x in need or (x != u and qs[x] in used):
                    go.add(x)
                    need |= dset[x]
                    if qs[x]:
                        used.add(qs[x])
            return None if u in go else order[:a] + [x for x in seg if x in go] + [x for x in seg if x not in go] + order[b + 1:]
        go, used = {u}, set()
        for x in seg[1:]:
            if dset[x] & go or (x != v and qs[x] in used):
                go.add(x)
                if qs[x]:
                    used.add(qs[x])
        return None if v in go else order[:a] + [x for x in seg if x not in go] + [x for x in seg if x in go] + order[b + 1:]

    seed = [PAR["seed"]]

    def draw(k):
        seed[0] = (seed[0] * 1103515245 + 12345) % 2147483648
        return (seed[0] >> 8) % k

    unit = [PAR["weights"][k] / max(run(order, k)) for k in range(len(sets))]
    live = [k for k, u in enumerate(unit) if u]

    def score(o, a, old):
        total, new = 0.0, []
        for m, k in enumerate(live):
            c, hold, wake = sets[k]
            late, soon = abs(wake), -min(wake, 0.0)
            fin, marks = old[m][0][:], old[m][1][:a // 32 + 1]
            free = marks[-1][:]
            for b in range(a // 32 * 32, n, 32):
                for i in o[b:b + 32]:
                    s = 0.0
                    for d in deps[i]:
                        if fin[d] > s:
                            s = fin[d]
                    q = qs[i]
                    if q:
                        s = s + late if s + soon > free[q] else free[q]
                        free[q] = s + hold[i]
                    elif land[i]:
                        s = 0.0
                    fin[i] = s + c[i]
                marks.append(free[:])
            total += unit[k] * max(fin)
            new.append((fin, marks))
        return total / sum(PAR["weights"]), new

    now, state = score(order, 0, [([0.0] * n, [[0.0] * 6]) for k in live])
    best, keep = now, order
    crit = pairs(order, 0)
    for r in range(rounds):
        u, v = crit[draw(len(crit))]
        back, k = draw(2), max(0, draw(5) - 1)
        if k:
            same = [x for x in order if qs[x] == qs[u]]
            if back:
                u = same[max(0, same.index(u) - k)]
            else:
                v = same[min(len(same) - 1, same.index(v) + k)]
        o = move(order, u, v, back)
        if o is None:
            continue
        s, new = score(o, order.index(u), state)
        if s <= now - PAR["heat"] * (1 - r / rounds) * math.log((1 + draw(4096)) / 4096):
            order, now, state = o, s, new
            crit = pairs(order, live[draw(len(live))])
            if s < best:
                best, keep = s, o
    return keep


SEMOF = {"V": "vec", "S": "act", "P": "ten", "G": "gps"}


def emit(g, T, ops, order):
    eng = {"V": g.vector, "S": g.scalar, "P": g.tensor, "G": g, "Y": g.sync}
    cnt = {"vec": 0, "act": 0, "ten": 0, "gps": 0}
    seen = {q: {} for q in eng}
    tok = {}
    for i in order:
        o = ops[i]
        if o["q"] == "X":
            tok[i] = (o["sem"][0], o["sem"][1], {o["sem"][0]: o["sem"][1]})
            continue
        q = o["q"]
        s = seen[q]
        toks = sorted([tok[d] for d in o["deps"] if tok.get(d) is not None], key=lambda x: (-sum(x[2].values()), x[0]))
        top = {}
        for sem, val, clock in toks:
            top[sem] = max(top.get(sem, 0), val)
        for sem, val, clock in toks:
            if s.get(sem, 0) >= val or top[sem] > val:
                continue
            eng[q].wait_ge(T.sem[sem], val)
            for k, w in clock.items():
                s[k] = max(s.get(k, 0), w)
        r = o["fn"]()
        tok[i] = None
        if o["kind"] == "c":
            sem = SEMOF[q]
            cnt[sem] += 1
            r.then_inc(T.sem[sem], 1)
            c = dict(s)
            c[sem] = cnt[sem]
            tok[i] = (sem, cnt[sem], c)
        elif o["kind"] == "dma":
            r.then_inc(T.sem[o["sem"]], 16)
    for sem in sorted(cnt):
        g.wait_ge(T.sem[sem], cnt[sem])


def rank_program(g, core, T, topo):
    rank = T.rank_of(core)
    if rank is None:
        return
    ops, nloc = build(g, T, topo, core, rank)
    if "order" not in LAY:
        LAY["order"] = arrange(ops, PAR["rounds"])
    emit(g, T, ops, LAY["order"])
    for k in range(len(PAR["out"])):
        g.wait_ge(T.sem["st%d" % k], 16)
    g.wait_ge(T.sem.stc, 16)
    g.wait_ge(T.sem.stl, 16)
    g.wait_ge(T.sem.loc, nloc[0])
